import numpy as np, ml_dtypes
CORES = [36,164,52,180,100,228,116,244]
N = 8
BF = ml_dtypes.bfloat16
W, H, P, RO, ST, TH = 2560, 1024, 256, 5, 3, 34
def place(o, i):
    return o[np.arange(8)[None, :, None, None], i]
def ground(rng):
    o = np.argsort(rng.random((8, W)), axis=-1); x = np.zeros((N, 8, 16, W), np.int64); top = np.zeros(8, np.int64)
    for g in range(8):
        m = int(rng.choice(np.array([3, 5, 8]))); c = rng.integers(0, 16, (m, 16)); s = np.linspace(0, m, W, endpoint=False)
        i = np.minimum(s.astype(np.int64), m - 1); f = (s - i)[:, None]
        b = np.rint(c[i] * (1 - f) + c[(i + 1) % m] * f).astype(np.int64).T
        y = b[None] + rng.integers(-1, 2, (N, 16, W))
        y = np.where(rng.random((N, 1, W)) < 0.03, rng.integers(0, 16, (N, 16, W)), y)
        x[:, g] = np.clip(y, 0, 15)[:, :, np.argsort(o[g])]; top[g] = W * 28 // (85 * m)
    return o, top, x
def knot(rng, r, share):
    k = (N, 8, 1, r.shape[3]); p = rng.integers(0, 15, k); q = np.minimum(p + rng.integers(1, 5, k), 15)
    hit = (rng.random(k) < share) & (np.arange(16)[None, None, :, None] == q)
    return np.where(hit, np.take_along_axis(r, p, 2), r)
def walk(rng, o, top, n):
    st = np.floor((rng.random((N, 8, 15, n)) * 1.2 - 0.2) * top[None, :, None, None]).astype(np.int64)
    st = st + np.where(rng.random(st.shape) < 0.01, rng.integers(0, W, st.shape), 0)
    a = rng.integers(0, W, (N, 8, 1, n))
    return knot(rng, place(o, np.concatenate([a, a + np.add.accumulate(st, axis=2)], axis=2) % W), 0.4)
def ladder(rng, lev):
    pm = np.argsort(rng.random((8, 16)), axis=-1)
    return np.clip(lev[:, :, None, :] - 15 * pm[None, :, :, None], 0, 15)
def pack(x, c, r):
    return {"x": np.ascontiguousarray(x.reshape(N, 128, W)).astype(np.float32).astype(BF), "c0": np.ascontiguousarray(c.reshape(N, 128, H)).astype(np.int32),
            "r0": np.ascontiguousarray(r.reshape(N, 128, P)).astype(np.int32)}
def setup_inputs(rng):
    o, top, x = ground(rng)
    return pack(x, walk(rng, o, top, H), walk(rng, o, top, P))
def setup_inputs_ties(rng):
    o = np.argsort(rng.random((8, W)), axis=-1); cls = np.argsort(o, axis=-1) % 7
    cr = np.where(rng.random((N, 8, W)) < 0.04, rng.integers(0, 7, (N, 8, W)), cls[None])
    lev = np.array([0, 1, TH, TH + 1, 2 * TH, 2 * TH + 1, 3 * TH + 2])[cr]
    def some(n):
        i = rng.integers(0, 6, (N, 8, n)); rows = [i]
        for p in range(15):
            jump = rng.random((N, 8, n)) < 0.04
            d = np.where(jump, rng.choice(np.array([-3, 3]), (N, 8, n)), rng.choice(np.array([-2, -2, -1, 0, 1, 2, 2]), (N, 8, n)))
            i = np.clip(i + d, 0, 5 + jump.astype(np.int64)); rows.append(i)
        i = np.stack(rows, axis=2)
        return place(o, i + 7 * rng.integers(0, W // 7, i.shape))
    return pack(ladder(rng, lev), some(H), some(P))
def setup_inputs_clash(rng):
    hi = np.arange(W - 64, W); last6 = (hi[:, None] * hi[None, :]) % 64 == 63; over = last6 & (hi[:, None] * (hi[None, :] + 64) > 2 ** 24)
    hu, hv = np.nonzero(over if np.any(over) else last6)
    nm = rng.random((8, W)) < 0.5; a = rng.integers(1, H - 1, 8); row = np.arange(16)[None, :, None]
    r = np.zeros((N, 8, 16, P), np.int64); c = np.zeros((N, 8, 16, H), np.int64); lev = np.zeros((N, 8, W), np.int64)
    for g in range(8):
        sp = np.array([0, H - 1, int(a[g]), int(a[g]) + H]); nm[g, sp] = True
        apart = rng.permutation(H)[:P] + H * rng.integers(0, 2, P)
        if g == 4: nm[g, apart] = True
        if g == 5: nm[g, W - 64:] = True
        ne, fa = np.flatnonzero(nm[g]), np.flatnonzero(~nm[g])
        if g < 2: u, v = sp[2:], np.array([0, 0])
        elif g < 4: u, v = sp[:2], np.array([int(rng.choice(ne)), 0])
        elif g == 4: u, v = apart, np.zeros(P, np.int64)
        elif g == 5: u, v = hi[hu], hi[hv]
        else: u, v = rng.choice(ne, 8), rng.choice(ne, 8)
        i = rng.integers(0, len(u), (N, P)); k = rng.integers(0, 16, (N, P))
        if g == 4: i = np.argsort(rng.random((N, P)), axis=-1)
        if g == 1 or g == 4: k = rng.integers(0, 14, (N, P))
        if g == 0: k[0, :3] = 15; k[0, 3] = 5; k[1] = 15; k[1, P - 1] = 3
        k[2] = np.minimum(k[2], 14)
        at = np.where(k < 15, k, rng.integers(0, 15, (N, P)))
        y = np.where(row > k[:, None], rng.choice(fa, (N, 16, P)), rng.choice(ne, (N, 16, P)))
        y = np.where(row == at[:, None], u[i][:, None], y)
        y[:, 15] = np.where(k == 14, y[:, 15], v[i]); r[:, g] = y
        flip = rng.random((N, W)) < 0.02; flip[:, sp] = False; flip[:3] = False
        lev[:, g] = np.where(nm[g][None] ^ flip, 0, 150) + rng.integers(0, 6, (N, W))
        c[:, g] = np.where(rng.random((N, 1, H)) < 0.5, rng.choice(ne, (N, 16, H)), rng.integers(0, W, (N, 16, H)))
    return pack(ladder(rng, lev), c, r)
def setup_inputs_loops(rng):
    o, top, x = ground(rng); x[:, ::2] = rng.integers(0, 3, (N, 4, 16, W))
    e = np.argsort(o, axis=-1); b = 1 + 2 * int(rng.integers(0, 4)); z = int(rng.integers(0, N))
    x[:, b] = np.where(e[b] % 3 == 0, rng.integers(0, 3, (N, 16, W)), x[:, b])
    def tie(r):
        kd = rng.integers(0, 8, (N, 8, r.shape[3]))
        for p in range(1, 16):
            r[:, :, p] = np.where(kd == 1, r[:, :, 0], r[:, :, p])
            if p > 1: r[:, :, p] = np.where(kd == 7, r[:, :, p % 2], r[:, :, p])
        for m, dst, src in ((2, 15, 0), (3, 15, 14), (4, 5, 0), (4, 9, 0), (5, 4, 1), (5, 6, 2), (6, 12, 3), (6, 8, 5)):
            r[:, :, dst] = np.where(kd == m, r[:, :, src], r[:, :, dst])
        return r
    w = walk(rng, o, top, P); w[z, b] = o[b][e[b][w[z, b]] // 3 * 3]
    return pack(x, tie(walk(rng, o, top, H)), tie(w))
def setup_inputs_calm(rng):
    o, top, x = ground(rng); q = rng.permutation(N)
    x[q[0]] = rng.integers(0, 3, (8, 16, W)); x[q[1]] = 15 * rng.integers(0, 2, (8, 16, W))
    x[:, int(rng.integers(0, 8))] = rng.integers(0, 3, (N, 16, W))
    e = np.argsort(o, axis=-1); home = e[None] % N == np.arange(N)[:, None, None]
    x = np.where(home[:, :, None], rng.integers(0, 3, x.shape), x)
    i = place(e, walk(rng, o, top, P)) // N * N + np.arange(N)[:, None, None, None]
    return pack(x, walk(rng, o, top, H), place(o, np.where(i < W, i, i - N)))
def setup_inputs_spread(rng):
    o = np.argsort(rng.random((8, W)), axis=-1); e = np.argsort(o, axis=-1) % 5
    x = np.floor(rng.random((N, 8, 16, W)) * np.exp2(4.0 - e)[None, :, None, :]).astype(np.int64)
    def some(n):
        k = rng.integers(0, 4, (N, 8, 1, n)); u = rng.random((N, 8, 16, n)); b = 5 * np.floor(u * (W // 5)).astype(np.int64)
        i = np.where(k == 0, np.floor(W * u).astype(np.int64), np.floor(W * u ** 4).astype(np.int64))
        i = np.where(k == 2, b + rng.integers(3, 5, u.shape), np.where(k == 3, b + rng.integers(2, 5, u.shape), i))
        return place(o, np.minimum(i, W - 1))
    return pack(x, some(H), some(P))
def check_inputs(d):
    bad = []; a = np.asarray(d["x"]).astype(np.float32)
    if not np.all((a >= 0) & (a <= 15) & (a == np.floor(a))): bad.append("whole numbers of x")
    for k in ("c0", "r0"):
        if np.min(d[k]) < 0 or np.max(d[k]) > W - 1: bad.append("range of " + k)
    return bad
def look(xs, R):
    return np.take_along_axis(xs, R.reshape(N, 8, 1, 16 * P), axis=3).reshape(N, 8, 16, 16, P)
def far(v, d):
    return np.add.reduce(np.abs(v[:, :, :, :16 - d] - v[:, :, :, d:]), axis=2)
def first(bad):
    return np.where(np.any(bad, axis=2), np.argmax(bad, axis=2), 15)[:, :, None, :]
def reference(x, c0, r0):
    xs = x.astype(np.float32).astype(np.int32).reshape(N, 8, 16, W); C = c0.astype(np.int64).reshape(N, 8, 16, H).copy()
    R = r0.astype(np.int64).reshape(N, 8, 16, P)
    kap = np.zeros(N, np.int64); row = np.arange(16)[None, None, :, None]
    for rnd in range(RO):
        if rnd > 0: R = np.roll(R, ST, axis=0)
        bad = far(look(xs, R), 1) > TH; fail = np.any(bad, axis=2); k = first(bad)
        rk = np.take_along_axis(R, k, 2)[:, :, 0]
        h = (((rk * R[:, :, 15]) >> 6) + rk + kap[:, None, None]) & (H - 1)
        R = np.where((row > k) & (row < 15), np.take_along_axis(C, h[:, :, None, :], 3), R)
        same = R[:, :, :, None] == R[:, :, None]
        q = 15 - np.argmax(same[:, :, :, ::-1], axis=3)
        p = first((q > row)[:, :, :15])
        R = np.where((row >= p) & (row <= np.take_along_axis(q, p, 2)), np.take_along_axis(R, p, 2), R)
        v = look(xs, R); k2 = first(far(v, 1) > TH)
        S = np.where((row > k2) & (row < 15), np.take_along_axis(R, k2, 2), R)
        for j in range(P - 1, -1, -1):
            a, g = np.nonzero(fail[:, :, j])
            C[a, g, :, h[a, g, j]] = S[:, :, :, j][a, g]
        near = far(v, 2) <= TH; R = R.copy()
        R[:, :, 1:14:2] = np.where(near[:, :, 0:13:2], R[:, :, 0:13:2], R[:, :, 1:14:2])
        kap = np.add.reduce(fail.astype(np.int64), axis=(1, 2))
    return {"yc": C.reshape(N, 128, H).astype(np.float32), "yr": R.reshape(N, 128, P).astype(np.float32)}

@@ -1,0 +1,549 @@
+from concourse.bass import DstId, RemoteDMATransfer
+from concourse.mybir import dt, AluOpType as A, AxisListType, ActivationFunctionType as F
+
+NC = 4
+n = 256 // NC
+NL = n // 16
+ROUNDS = 5
+CW = 1408
+MODE1 = "MAMA"
+MODE2 = "MAMA"
+HG = 2
+
+SCRATCH = {
+    "xw": ("sbuf", [128, 2560], "bfloat16"), "ri": ("sbuf", [128, 256], "int32"), "ci": ("sbuf", [128, 1024], "int32"),
+    "cc": ("sbuf", [128, CW], "float32"), "cy": ("sbuf", [128, CW], "float32"), "iot": ("sbuf", [128, 1024], "float32"),
+    "rf": ("sbuf", [128, 256 * ROUNDS], "float16"), "sd": ("sbuf", [128, 256 * ROUNDS], "float16"),
+    "rl": ("sbuf", [128, 512], "uint16"), "rls": ("sbuf", [128, 512], "uint16"),
+    "rl2": ("sbuf", [128, 512], "uint16"), "rls2": ("sbuf", [128, 512], "uint16"),
+    "v1": ("sbuf", [128, 4096], "bfloat16"), "m1": ("sbuf", [128, 4096], "bfloat16"),
+    "v2": ("sbuf", [128, 4096], "bfloat16"), "m2": ("sbuf", [128, 4096], "bfloat16"), "ad": ("sbuf", [128, 2048], "bfloat16"),
+    "f": ("sbuf", [128, 512], "float16"), "q": ("sbuf", [128, 512], "float16"), "mk": ("sbuf", [128, 512], "float16"),
+    "rn": ("sbuf", [128, 512], "float16"), "cm": ("sbuf", [128, 512], "float16"), "r2": ("sbuf", [128, 512], "float16"),
+    "em": ("sbuf", [128, 4096], "float16"), "hd": ("sbuf", [128, 512], "float16"), "g1": ("sbuf", [128, 512], "float16"),
+    "qd": ("sbuf", [128, 512], "float16"), "eq": ("sbuf", [128, 512], "float16"), "ins": ("sbuf", [128, 512], "float16"),
+    "t3": ("sbuf", [128, 512], "float32"), "r3": ("sbuf", [128, 512], "float16"), "r3c": ("sbuf", [128, 512], "float32"),
+    "fs": ("sbuf", [128, 1024], "float16"), "fz": ("sbuf", [128, 1024], "float16"), "nr": ("sbuf", [128, 512], "float16"),
+    "t4": ("sbuf", [128, 512], "float32"), "q5": ("sbuf", [128, 512], "float16"), "k5": ("sbuf", [128, 512], "float16"),
+    "t5": ("sbuf", [128, 512], "float32"), "yo": ("sbuf", [128, 256], "float32"),
+    "rr": ("sbuf", [128, 16 * ROUNDS], "float32"), "q15": ("sbuf", [128, 256], "float16"),
+    "w": ("sbuf", [128, 32], "float32"), "hi": ("sbuf", [128, 32], "int32"), "hj": ("sbuf", [128, 32], "int32"),
+    "hl": ("sbuf", [128, 32], "uint16"), "nf": ("sbuf", [128, 32], "float32"), "hf": ("sbuf", [128, 32], "float32"),
+    "hr": ("sbuf", [128, 512], "float16"), "EQ": ("sbuf", [128, 16, 256], "float16"), "TRI": ("sbuf", [128, 16, 16], "float16"),
+    "lz": ("sbuf", [128, 256], "float16"), "lx": ("sbuf", [128, 16], "float32"), "lo": ("sbuf", [128, 16], "float32"),
+    "tj": ("sbuf", [128, 16], "float32"), "th": ("sbuf", [128, 16], "float32"), "tm": ("sbuf", [128, 16], "float32"),
+    "ts": ("sbuf", [128, 16], "float32"), "off": ("sbuf", [128, 32], "uint16"),
+    "kc": ("sbuf", [128, ROUNDS], "float32"), "kj": ("sbuf", [128, 64], "float32"),
+    "col": ("sbuf", [128, 8], "float32"), "one": ("sbuf", [128, 128], "bfloat16"),
+    "B8": ("sbuf", [128, 1024], "bfloat16"), "UP": ("sbuf", [128, 1024], "bfloat16"), "UC": ("sbuf", [128, 1024], "bfloat16"),
+    "DD": ("sbuf", [128, 1024], "bfloat16"), "MM": ("sbuf", [128, 1024], "bfloat16"),
+    "W2": ("sbuf", [128, 2048], "bfloat16"), "NW": ("sbuf", [128, 2048], "bfloat16"), "Q": ("sbuf", [128, 16], "bfloat16"),
+}
+for _k in ("B", "B0", "I", "L", "SH", "SD", "LI", "UI", "US", "LP", "ZN", "ZA", "ZT", "IT", "IK", "I2", "I16", "NI", "NH", "YA",
+           "DS", "R15", "C2", "C19"):
+    SCRATCH[_k] = ("sbuf", [128, 128], "bfloat16")
+for _k in range(8):
+    SCRATCH["b%d" % _k] = ("psum", [128, 512], "float32")
+SEMAPHORES = ["v", "s", "p", "q", "sent", "ar", "dr", "dx", "dc", "oy0", "oy1", "oc"] + \
+    ["a%d_%d" % (t, c) for t in range(1, ROUNDS) for c in range(NC)]
+WIDE = set(k for k in SCRATCH if SCRATCH[k][2] in ("float32", "int32"))
+
+CY, PE, GA, WAKE, OWN, NET = 0.001, 0.0005, 1.5, 0.12, 0.06, 3.0
+
+
+def R(name, a, b, step=1):
+    return (name, a, b, (slice(None), slice(a, b, step)))
+
+
+def size(r):
+    s = r[3][-1]
+    return 256 if len(r) > 4 else len(range(s.start, s.stop, s.step or 1))
+
+
+def ind(win, off):
+    return ("ind", win, off)
+
+
+def isref(x):
+    return isinstance(x, tuple)
+
+
+def make_plan():
+    ops = []
+
+    def op(queue, kind, args, reads, writes, cost, **kw):
+        d = dict(i=len(ops), q=queue, kind=kind, args=args, r=[], w=list(writes), cost=cost, sem=None)
+        for x in reads:
+            if isref(x):
+                d["r"] += [x[1], x[2]] if x[0] == "ind" else [x]
+        d.update(kw)
+        ops.append(d)
+        return d
+
+    def boost(x, o):
+        o["pb"] = x
+
+    two = lambda r: r[0] not in WIDE and r[0][0] != "b"
+
+    def ts(out, in0, s1, s2=None, op0=A.add, op1=None):
+        c = max(64, size(in0) * (0.5 if two(out) and two(in0) else 1)) * CY
+        return op("v", "ts", (out, in0, s1, s2, op0, op1), [in0, s1, s2], [out], c)
+
+    def tt(out, in0, in1, o):
+        if out[0] == "ind":
+            return op("v", "tt", (out, in0, in1, o), [in0, in1, out[2]], [out[1]], 0.05 + size(in0) * 3 * CY)
+        if in0[0] == "ind":
+            c = 0.05 + size(in1) * GA * CY
+        else:
+            c = max(64, size(in0) * (1 if in0[0][0] == "b" or in1[0][0] == "b" else 2)) * CY
+        return op("v", "tt", (out, in0, in1, o), [in0, in1], [out], c)
+
+    def cp(out, in_):
+        k = size(out)
+        return op("v", "cp", (out, in_), [in_], [out], 0.05 + k * GA * CY if in_[0] == "ind" else max(64, k) * CY)
+
+    def ms(out, val):
+        return op("v", "ms", (out, val), [], [out], max(64, size(out) * (.5 if two(out) else 1)) * CY)
+
+    def act(out, in_, fn, bias=0.0, scale=1.0, acc=None):
+        k = size(out)
+        return op("s", "act", (out, in_, fn, bias, scale, acc), [in_], [out] + ([acc] if acc else []),
+                  (0.065 + k * GA * CY) if in_[0] == "ind" else max(64, k) * CY)
+
+    def K(name):
+        return R(name, 0, 128)
+
+    def grp(out, *pairs):
+        last = len(pairs) - 1
+        return [(out, K(a) if isinstance(a, str) else a, b, i == 0, i == last) for i, (a, b) in enumerate(pairs)]
+
+    def mm(*mms):
+        rd = []
+        for m in mms:
+            rd += [m[1], m[2]]
+        return op("p", "mm", mms, rd, sorted(set((m[0][0], m[0][1], m[0][2]) for m in mms)), sum(max(64, size(m[2])) for m in mms) * PE)
+
+    def iota(out, pat, base, cm):
+        return op("q", "iota", (out, pat, base, cm), [K("SH")], [out], 0.13 + 2 * size(out) * CY)
+
+    def sel(out, in_, pat, cmp, fill, base, cm):
+        return op("q", "sel", (out, in_, pat, cmp, fill, base, cm), [in_], [out], 0.17 + 2 * size(out) * CY)
+
+    def dma(sem, out, in_, reads, writes, cost):
+        return op("y", "dma", (out, in_), reads, writes, cost, sem=sem)
+
+    dma("dr", R("ri", 0, 256), ("T", "r0"), [], [R("ri", 0, 256)], 2.2)
+    dma("dx", R("xw", 0, 2560), ("T", "x"), [], [R("xw", 0, 2560)], 5.0)
+    dma("dc", R("ci", 0, 1024), ("T", "c0"), [], [R("ci", 0, 1024)], 7.5)
+    IN = [[-16, 8], [-1, 16]]
+    boost(1000, ms(K("one"), 1.0))
+    sel(K("B0"), K("one"), [[-16, 8], [0, 16]], A.is_ge, 0.0, 0, 1)
+    sel(K("B"), K("B0"), [[16, 8], [0, 16]], A.is_ge, 0.0, 15, -1)
+    boost(200, sel(K("I"), K("B"), IN, A.is_equal, 0.0, 0, 1))
+    boost(100, sel(K("SH"), K("B"), IN, A.is_equal, 0.0, -1, 1))
+    ms(R("W2", 0, 2048), 0.0)
+    boost(90, sel(K("L"), K("B"), [[16, 8], [1, 16]], A.is_gt, 0.0, 0, -1))
+    sel(K("SD"), K("B"), IN, A.is_equal, 0.0, 1, 1)
+    for p in range(16):
+        a = 128 * p
+        ts(("W2", a, a + 128, (slice(None), slice(a + p, a + 128, 16))), R("B", 0, 128, 16), 2.0, None, A.mult)
+    act(K("NI"), K("I"), F.Copy, scale=-1.0)
+    act(K("NH"), K("I"), F.Copy, scale=-0.5)
+    for i in range(4):
+        a = 512 * i
+        o = R("b%d" % i, 0, 512)
+        if i:
+            mm(*grp(o, ("NH", R("W2", a, a + 512)), ("NH", R("W2", a - 128, a + 384))))
+        else:
+            mm(*(grp(R("b0", 0, 128), ("NH", R("W2", 0, 128))) +
+                 grp(R("b0", 128, 512), ("NH", R("W2", 128, 512)), ("NH", R("W2", 0, 384)))))
+        act(R("NW", a, a + 512), o, F.Copy)
+    for c in range(NC):
+        ts(R("rf", c * n, c * n + n), R("ri", c * n, c * n + n), -1280.0)
+    op("v", "red", (R("col", 0, 1), R("I", 15, 128, 16)), [R("I", 15, 128, 16)], [R("col", 0, 1)], .07)
+    op("v", "red", (R("col", 1, 2), R("I", 1, 128, 2)), [R("I", 1, 128, 2)], [R("col", 1, 2)], .07)
+    tt(R("col", 2, 3), R("col", 1, 2), R("col", 0, 1), A.subtract)
+    ts(R("col", 3, 4), R("col", 2, 3), 3.5, -1.0, A.mult, A.add)
+    ts(R("q15", 0, 256), R("rf", 0, 256), R("col", 0, 1), None, A.mult)
+    mm(*grp(R("b4", 256, 272), *[(R("W2", 128 * j, 128 * j + 128), R("q15", j, 256, 16)) for j in range(16)]))
+    ts(R("rr", 0, 16), R("b4", 256, 272), 1.0 / 256, 10.5, A.mult, A.add)
+    op("q", "rsend", (), [R("rr", 0, 16)], [], 1.5)
+    op("n", "arr", (), [], [R("rr", 16, 16 * ROUNDS)], 0.0, sem="ar", tdep=(ops[-1], NET))
+    act(K("ZT"), K("L"), F.Copy, scale=-16384.0)
+    act(K("ZA"), K("I"), F.Copy, scale=8192.0)
+    tt(K("ZA"), K("ZA"), K("ZT"), A.add)
+    act(K("LP"), K("L"), F.Copy)
+    act(R("LP", 15, 128, 16), R("I", 15, 128, 16), F.Copy, scale=0.0)
+    act(K("ZN"), K("LP"), F.Copy, scale=-8192.0)
+    act(K("IT"), K("I"), F.Copy)
+    act(R("IT", 15, 128, 16), R("I", 15, 128, 16), F.Copy, scale=0.0)
+    act(K("IK"), K("IT"), F.Copy, scale=1280.0)
+    ms(K("C2"), 320.0)
+    ms(("C2", 0, 128, (slice(0, 1), slice(0, 128))), 318.0)
+    ms(K("C19"), 150.0)
+    ms(("C19", 0, 128, (slice(0, 1), slice(0, 128))), 149.0)
+    ms(R("kc", 0, 1), -0.4921875)
+    ts(R("cc", 0, 1024), R("ci", 0, 1024), -1280.0)
+    ms(R("cc", 1024, CW), 0.0)
+    ms(R("cy", 1024, CW), 0.0)
+    for h in range(8):
+        ts(R("B8", 128 * h, 128 * h + 128), K("B"), 1.0, None, A.mult)
+    sel(R("UP", 0, 1024), R("B8", 0, 1024), [[-1, 8], [-16, 8], [-1, 16]], A.is_equal, 0.0, -1, 1)
+    sel(R("UC", 0, 1024), R("B8", 0, 1024), [[1, 8], [-16, 8], [-1, 16]], A.is_equal, 0.0, -15, 1)
+    T1 = lambda nm, s: R(nm, 128 * s, 128 * s + 128)
+    for h in range(2):
+        o = "b%d" % (6 + h)
+        mm(*sum([grp(T1(o, i), ("I", T1("UP", 4 * h + i)), (T1("UC", 4 * h + i), K("I")), ("NI", K("I"))) for i in range(4)], []))
+        act(R("DD", 512 * h, 512 * h + 512), R(o, 0, 512), F.Copy)
+    for h in range(2):
+        o = "b%d" % (6 + h)
+        mm(*sum([grp(T1(o, i), (T1("UP", 4 * h + i), T1("UP", 4 * h + i)), ("I", T1("UC", 4 * h + i))) for i in range(4)], []))
+        act(R("MM", 512 * h, 512 * h + 512), R(o, 0, 512), F.Copy)
+    tt(K("LI"), K("L"), K("I"), A.add)
+    tt(K("UI"), K("B"), K("L"), A.subtract)
+    tt(K("US"), K("B"), K("LI"), A.subtract)
+    act(K("I2"), K("I"), F.Copy, scale=2.0)
+    act(K("I16"), K("I"), F.Copy, scale=16.0)
+    tt(K("YA"), K("I"), K("SD"), A.add)
+    tt(K("DS"), K("SD"), K("I"), A.subtract)
+    ts(K("R15"), K("one"), R("col", 0, 1), None, A.mult)
+    iota(R("iot", 0, 1024), [[1, 1024]], 0, 0)
+    iota(R("tj", 0, 16), [[16, 16]], 1024, 1)
+
+    X = R("xw", 0, 2560)
+    sends = {}
+    for t in range(ROUNDS):
+        P2 = 256 * (t % 2)
+        last = t == ROUNDS - 1
+
+        def G(name, c, k=n):
+            a = (P2 // 64) * (k * NC // 4) + k * c
+            return R(name, a, a + k)
+
+        def b(c, i, k=n):
+            return R("b%d" % c, 64 * i, 64 * i + k)
+
+        def lw(name, c):
+            return R(name, 16 * (t % 2) + NL * c, 16 * (t % 2) + NL * c + NL)
+
+        def distances(c, rin, rl, rls, vb, mb, tile, mode):
+            v0 = 1024 * c
+            if mode == "M":
+                mm(*grp(b(c, 0), ("SH", rin)))
+                ts(rls, b(c, 0), 1280.0)
+            for h in range(HG):
+                w = 1024 // HG
+                vh, u, z = R(vb, v0 + w * h, v0 + w * h + w), n // HG * h, n // HG * h + n // HG
+                act(vh, ind(X, R(rl[0], rl[1] + u, rl[1] + z)), F.Copy)
+                if mode == "M":
+                    tt(R(mb, v0 + w * h, v0 + w * h + w), ind(X, R(rls[0], rls[1] + u, rls[1] + z)), vh, A.max)
+            red = [(R("W2", 128 * p, 128 * p + 128), R(mb, v0 + p, v0 + 1024, 16)) for p in range(15)]
+            if mode == "M":
+                red += [(R("NW", 128 * p, 128 * p + 128), R(vb, v0 + p, v0 + 1024, 16)) for p in range(16)]
+            else:
+                for h in range(2):
+                    e = "b%d" % (6 + (c + h) % 2)
+                    a = v0 + 512 * h
+                    mm(*grp(R(e, 0, 511), ("I", R(vb, a + 1, a + 512)), ("NI", R(vb, a, a + 511))))
+                    act(R(mb, a, a + 511), R(e, 0, 511), F.Abs, scale=0.5)
+            return grp(R("b%d" % (4 + c % 2), 64 * tile, 64 * tile + n), *red)
+
+        for c in range(NC):
+            rin = R("rf", 256 * t + n * c, 256 * t + n * c + n)
+            if t:
+                op("n", "arr", (), [], [rin], 0.0, sem="a%d_%d" % (t, c), tdep=(sends[t - 1, c], NET))
+            ts(G("rl", c), rin, 1280.0)
+            mm(*distances(c, rin, G("rl", c), G("rls", c), "v1", "m1", 0, MODE1[c]))
+            ts(G("f", c), R("b%d" % (4 + c % 2), 0, n), 34.5, None, A.is_gt)
+            mm(*(grp(b(c, 1), ("I", rin), ("ZA", G("f", c))) + grp(b(c, 2), ("I", rin), ("ZN", G("f", c)))))
+            ts(G("q", c), b(c, 1), 6911.0, -8191.0, A.max, A.add)
+            q0 = G("q", c)[1]
+            mm(*grp(b(c, 3, NL), ("C2", R("one", 0, NL)),
+                    *[(R("W2", 128 * j, 128 * j + 128), R("q", q0 + j, q0 + n, 16)) for j in range(16)]))
+            tt(lw("w", c), b(c, 3, NL), R("rr", 16 * t + NL * c, 16 * t + NL * c + NL), A.mult)
+            ts(lw("hi", c), lw("w", c), R("kc", t, t + 1))
+            ts(lw("hj", c), lw("hi", c), 1023, None, A.bitwise_and)
+            cp(lw("hl", c), lw("hj", c))
+            ts(lw("nf", c), b(c, 3, NL), -1.0, -4096.0, A.is_lt, A.mult)
+            ts(G("mk", c), b(c, 1), -1280.5, None, A.is_lt)
+            ts(G("rn", c), b(c, 2), -1280.0, None, A.max)
+            tt(G("cm", c), ind(R("cc", 0, 1024), lw("hl", c)), G("mk", c), A.mult)
+            mm(*grp(b(c, 4), ("I", G("rn", c)), ("IK", G("mk", c)), ("IT", G("cm", c))))
+            ts(G("rl2", c), b(c, 4), 1280.0)
+            ts(G("r2", c), b(c, 4), 0.0)
+        if t == 0:
+            ms(R("Q", 0, 16), 0.0)
+            for e in range(8):
+                sel(R("Q", 0, 16), R("Q", 0, 16), [[-1, 16]], A.not_equal, 1.0, -16 * e, 1)
+            mm(*grp(R("b4", 288, 304), ("US", R("Q", 0, 16))))
+            for j in range(16):
+                act(("TRI", 16 * j, 16 * j + 16, (slice(None), j, slice(0, 16))), R("b4", 288, 304), F.Copy)
+        for c in range(NC):
+            e = "b%d" % (6 + c % 2)
+            mm(*sum([grp(R(e, n * s, n * s + n), (T1("DD", s), G("r2", c))) for s in range(8)], []))
+            em = R("em", 2 * 1024 * (t % 2) + 512 * c, 2 * 1024 * (t % 2) + 512 * c + 512)
+            ts(em, R(e, 0, 512), 0.0, None, A.is_equal)
+            D1 = distances(c, G("r2", c), G("rl2", c), G("rls2", c), "v2", "m2", 1, MODE2[c])
+            v0 = 1024 * c
+            mm(*grp(R(e, 0, 511), ("I", R("v2", v0 + 2, v0 + 1024, 2)), ("NI", R("v2", v0, v0 + 1022, 2))))
+            act(R("ad", 512 * c, 512 * c + 511), R(e, 0, 511), F.Abs, scale=0.5)
+            mm(*grp(b(c, 5), *[(T1("MM", s), R("em", em[1] + n * s, em[1] + n * s + n)) for s in range(8)]))
+            ts(G("hd", c), b(c, 5), 1.0, None, A.is_ge)
+            mm(*grp(b(c, 6), ("I", G("r2", c)), ("ZA", G("hd", c))))
+            ts(G("qd", c), b(c, 6), 6911.0, -8191.0, A.max, A.add)
+            ts(G("g1", c), b(c, 6), 4000.0, 64.0, A.is_gt, A.mult)
+            mm(*grp(b(c, 0), ("C19", R("one", 0, n)), ("NI", G("r2", c)), ("B", G("qd", c))))
+            ts(G("eq", c), b(c, 0), 0.0, None, A.is_equal)
+            mm(*(grp(b(c, 1), ("LI", G("g1", c)), ("US", G("eq", c))) + grp(b(c, 2), ("LI", G("g1", c)), ("UI", G("eq", c)))))
+            ts(G("ins", c), b(c, 2), 64.5, None, A.is_gt)
+            tt(G("t3", c), b(c, 0), G("ins", c), A.mult)
+            tt(G("r3", c), b(c, 4), G("t3", c), A.add)
+            mm(*D1)
+            D = "b%d" % (4 + c % 2)
+            mm(*grp(R(D, 128, 128 + n), *[(T1("W2", p + 1), R("ad", 512 * c + p // 2, 512 * c + 512, 8)) for p in range(0, 13, 2)]))
+            fs, fz = G("fs", c, 2 * n), G("fz", c, 2 * n)
+            ts(fs, R(D, 64, 64 + 2 * n), 34.5, 64.5, A.is_gt, A.mult)
+            tt(fz, fs, R("b%d" % c, 64, 64 + 2 * n), A.is_gt)
+            f2, F2 = R("fz", fz[1], fz[1] + n), R("fz", fz[1] + n, fz[1] + 2 * n)
+            mm(*(grp(b(c, 5), ("I2", G("ins", c)), ("YA", f2), ("I16", F2)) + grp(b(c, 6), ("DS", G("r3", c)))))
+            ts(G("nr", c), b(c, 5), R("col", 3, 4), None, A.is_lt)
+            tt(G("t4", c), b(c, 6), G("nr", c), A.mult)
+            if not last:
+                so = R("sd", 256 * t + n * c, 256 * t + n * c + n)
+                tt(so, G("r3", c), G("t4", c), A.add)
+                sends[t, c] = op("q", "send", (t, c), [so], [], 1.0)
+            act(G("r3c", c), G("r3", c), F.Identity if last else F.Copy, bias=1280.0 if last else 0.0)
+            if last:
+                tt(R("yo", n * c, n * c + n), G("r3c", c), G("t4", c), A.add)
+                if c % 2:
+                    x = n * (c - 1)
+                    dma("oy%d" % (c // 2), ("T", "yr", x, x + 2 * n), R("yo", x, x + 2 * n), [R("yo", x, x + 2 * n)], [], 2.0)
+            mm(*(grp(b(c, 7), ("I", G("r3", c)), ("ZA", f2)) + grp(b(c, 3), ("LP", f2))))
+            ts(G("q5", c), b(c, 7), 6911.0, -8191.0, A.max, A.add)
+            act(G("k5", c), b(c, 3), F.Sign)
+            mm(*grp(b(c, 0), ("C19", R("one", 0, n)), ("NI", G("r3", c)), ("B", G("q5", c))))
+            tt(G("t5", c), b(c, 0), G("k5", c), A.mult)
+            if c == 1:
+                if not last:
+                    mm(*grp(R("b5", 320, 384), *[("R15", G("mk", i)) for i in range(NC)]))
+                    act(R("kj", 0, 64), R("b5", 320, 384), F.Identity, bias=-0.4921875 / 64, acc=R("kc", t + 1, t + 2))
+                x = 16 * (t % 2)
+                H = lambda nm: R(nm, x, x + 16)
+                act(R("hr", 16 * x, 16 * x + 256), ind(R("iot", 0, 1024), H("hl")), F.Copy)
+                tt(H("hf"), H("hj"), H("nf"), A.add)
+                for j in range(16):
+                    z = 256 - 16 * j
+                    ts(("EQ", 256 * j, 256 * j + z, (slice(None), j, slice(0, z))), R("hr", 16 * x + 16 * j, 16 * x + 256),
+                       R("hf", x + j, x + j + 1), None, A.is_equal)
+                dg = ("EQ", 0, 4096, (slice(None), slice(0, 16), slice(0, 16)), 3)
+                tt(dg, dg, ("TRI", 0, 256, (slice(None), slice(0, 16), slice(0, 16)), 3), A.mult)
+                mm(*[(R("b4", 256 + 16 * j, 512), K("B"), ("EQ", 256 * j, 512 * j + 256 - 16 * j - 256 * j, (slice(None), j, slice(0, 256 - 16 * j))),
+                      j == 0, j == 15) for j in range(16)])
+                act(R("lz", 0, 256), R("b4", 256, 512), F.Sign)
+                mm(*grp(R("b5", 256, 272), *[(R("W2", 128 * j, 128 * j + 128), R("lz", j, 256, 16)) for j in range(16)]))
+                tt(R("lx", 0, 16), R("b5", 256, 272), H("nf"), A.subtract)
+                ts(R("lo", 0, 16), R("lx", 0, 16), 1.0, None, A.is_ge)
+                tt(R("th", 0, 16), R("tj", 0, 16), H("hj"), A.subtract)
+                tt(R("tm", 0, 16), R("lo", 0, 16), R("th", 0, 16), A.mult)
+                tt(R("ts", 0, 16), R("tm", 0, 16), H("hj"), A.add)
+                cp(H("off"), R("ts", 0, 16))
+                if last:
+                    act(R("cy", 0, 1024), R("cc", 0, 1024), F.Identity, bias=1280.0)
+        for c in range(NC):
+            tt(ind(R("cy" if last else "cc", 0, CW), lw("off", c)), G("t5", c), G("r3c", c), A.add)
+    dma("oc", ("T", "yc", 0, 1024), R("cy", 0, 1024), [R("cy", 0, 1024)], [], 4.0)
+    return ops
+
+
+def link(ops):
+    seen = {}
+    for o in ops:
+        dep = set()
+        acc = [(r, False) for r in o["r"]] + [(w, True) for w in o["w"]]
+        for r, wr in acc:
+            name, a, b = r[0], r[1], r[2]
+            ps = SCRATCH[name][0] == "psum"
+            for (x, y, pw, po) in seen.get(name, ()):
+                if po is not o and ((a < y and x < b and (wr or pw)) or (ps and po["q"] != o["q"])):
+                    dep.add(po["i"])
+        for r, wr in acc:
+            name, a, b = r[0], r[1], r[2]
+            keep = [e for e in seen.get(name, ()) if e[3] is o or not (wr and a <= e[0] and e[1] <= b)]
+            keep.append((a, b, wr, o))
+            seen[name] = keep
+        o["dep"] = sorted(dep)
+
+
+def schedule(ops):
+    N = len(ops)
+    succ = [[] for _ in range(N)]
+    need = [0] * N
+    for o in ops:
+        for d in o["dep"]:
+            succ[d].append((o["i"], OWN if ops[d]["q"] == o["q"] else WAKE))
+            need[o["i"]] += 1
+        if o.get("tdep"):
+            succ[o["tdep"][0]["i"]].append((o["i"], o["tdep"][1]))
+            need[o["i"]] += 1
+    pri = [0.0] * N
+    for i in range(N - 1, -1, -1):
+        pri[i] = ops[i]["cost"] + max([lat + pri[j] for j, lat in succ[i]] + [0.0])
+    pri = [x + o.get("pb", 0) for x, o in zip(pri, ops)]
+    est = [0.0] * N
+    ready = {}
+    for o in ops:
+        if not need[o["i"]]:
+            ready.setdefault(o["q"], []).append(o["i"])
+    free, busy, order = {}, {}, []
+    while len(order) < N:
+        best = None
+        for q, L in ready.items():
+            if L:
+                f = free.get(q, 0.0)
+                s = min(max(f, est[i]) for i in L)
+                if best is None or s < best[0]:
+                    best = (s, q)
+        s, q = best
+        f = free.get(q, 0.0)
+        i = max([i for i in ready[q] if max(f, est[i]) <= s + 1e-9], key=lambda k: (pri[k], -k))
+        ready[q].remove(i)
+        o = ops[i]
+        o["t0"] = s
+        end = s + o["cost"]
+        free[q] = s if o["kind"] == "arr" else (s + 0.05 if o["kind"] == "dma" else end)
+        busy[q] = busy.get(q, 0.0) + o["cost"]
+        order.append(i)
+        for j, lat in succ[i]:
+            est[j] = max(est[j], end + lat)
+            need[j] -= 1
+            if not need[j]:
+                ready.setdefault(ops[j]["q"], []).append(j)
+    return order, max(o["t0"] + o["cost"] for o in ops), busy
+
+
+def waits(ops, order):
+    cnt, know = {}, {}
+    for i in order:
+        o = ops[i]
+        q = o["q"]
+        kn = know.setdefault(q, {})
+        w = {}
+        for d in o["dep"]:
+            s, v = ops[d]["done"]
+            if kn.get(s, 0) < v and w.get(s, (0,))[0] < v:
+                w[s] = (v, d)
+        o["waits"] = []
+        for s in sorted(w, key=lambda k: -ops[w[k][1]]["t0"]):
+            v, d = w[s]
+            if kn.get(s, 0) >= v:
+                continue
+            o["waits"].append((s, v))
+            for a, z in ops[d]["snap"].items():
+                kn[a] = max(kn.get(a, 0), z)
+            kn[s] = max(kn.get(s, 0), v)
+        if o["kind"] in ("arr", "dma"):
+            o["done"] = (o["sem"], 16)
+        elif o["kind"] in ("send", "rsend"):
+            o["done"] = ("sent", 0)
+        else:
+            cnt[q] = cnt.get(q, 0) + 1
+            o["done"] = (q, cnt[q])
+        o["snap"] = dict(kn)
+    return cnt
+
+
+PLAN = {}
+
+
+def plan():
+    if not PLAN:
+        ops = make_plan()
+        link(ops)
+        order, total, busy = schedule(ops)
+        PLAN.update(ops=ops, order=order, cnt=waits(ops, order), total=total, busy=busy)
+    return PLAN
+
+
+def rank_program(g, core, T, topo):
+    rank = T.rank_of(core)
+    if rank is None:
+        return
+    pl = plan()
+    ops = pl["ops"]
+    N = len(T.cores)
+    queue = {"v": g.vector, "s": g.scalar, "p": g.tensor, "q": g, "y": g.sync}
+
+    def ap(r):
+        if not isref(r):
+            return r
+        if r[0] == "ind":
+            return ap(r[1]).indirect(ap(r[2]))
+        return T[r[0]][r[3]]
+
+    def side(r):
+        if r[0] == "T":
+            return T[r[1]][:, r[2]:r[3]] if len(r) > 2 else T[r[1]][:]
+        return ap(r)
+
+    nxt = T.cores[(rank + 3) % N]
+    sent = [0]
+    narr = {}
+    for t in range(1, ROUNDS):
+        for c in range(NC):
+            narr["a%d_%d" % (t, c)] = len(topo.engines(T.cores[(rank - 3) % N], core))
+    narr["ar"] = sum(len(topo.engines(T.cores[(rank - 3 * t) % N], core)) for t in range(1, ROUNDS))
+    for i in pl["order"]:
+        o = ops[i]
+        k, a = o["kind"], o["args"]
+        if k == "arr":
+            continue
+        Q = queue[o["q"]]
+        for s, v in o["waits"]:
+            Q.wait_ge(T.sem[s], narr.get(s, v))
+        if k == "ts":
+            r = Q.tensor_scalar(ap(a[0]), ap(a[1]), ap(a[2]), ap(a[3]), a[4]) if a[5] is None else \
+                Q.tensor_scalar(ap(a[0]), ap(a[1]), ap(a[2]), ap(a[3]), a[4], a[5])
+        elif k == "tt":
+            r = Q.tensor_tensor(ap(a[0]), ap(a[1]), ap(a[2]), a[3])
+        elif k == "cp":
+            r = Q.tensor_copy(ap(a[0]), ap(a[1]))
+        elif k == "ms":
+            r = Q.memset(ap(a[0]), a[1])
+        elif k == "red":
+            r = Q.tensor_reduce(ap(a[0]), ap(a[1]), AxisListType.X, A.add)
+        elif k == "act":
+            r = Q.activation(ap(a[0]), ap(a[1]), a[2], bias=ap(a[3]), scale=a[4], accum_out=ap(a[5]))
+        elif k == "mm":
+            for m in a:
+                r = Q.matmul(ap(m[0]), ap(m[1]), ap(m[2]), m[3], m[4])
+        elif k == "iota":
+            r = Q.iota(ap(a[0]), a[1], a[2], a[3], allow_small_or_imprecise_dtypes=True)
+        elif k == "sel":
+            r = Q.affine_select(ap(a[0]), ap(a[1]), a[2], a[3], a[4], a[5], a[6])
+        elif k == "dma":
+            Q.dma_start(side(a[0]), side(a[1])).then_inc(T.sem[o["sem"]], 16)
+            continue
+        elif k == "send":
+            rid, pid = topo.addr(nxt, core)
+            src = R("sd", 256 * a[0] + n * a[1], 256 * a[0] + n * a[1] + n)
+            dst = R("rf", 256 * (a[0] + 1) + n * a[1], 256 * (a[0] + 1) + n * a[1] + n)
+            Q.remote_dma(ap(dst), ap(src), T.sem["a%d_%d" % (a[0] + 1, a[1])], T.sem["sent"], pid, rid, topo.mask(core, nxt))
+            sent[0] += len(topo.engines(core, nxt))
+            continue
+        else:
+            ids, dsts = [], []
+            for t in range(1, ROUNDS):
+                d = T.cores[(rank + 3 * t) % N]
+                rid, pid = topo.addr(d, core)
+                ids.append(DstId(rid=rid, pnc=pid))
+                dsts.append(ap(R("rr", 16 * t, 16 * t + 16)))
+            Q.remote_dma_fused([RemoteDMATransfer(dst_ids=ids, dma_engine_mask=topo.mask(core, nxt), remote_sem=T.sem["ar"],
+                                                  srcs=[ap(R("rr", 0, 16))], dsts=dsts)], local_sem=T.sem["sent"])
+            sent[0] += len(topo.engines(core, nxt))
+            continue
+        r.then_inc(T.sem[o["q"]], 1)
+    for s in sorted(pl["cnt"]):
+        g.wait_ge(T.sem[s], pl["cnt"][s])
+    g.wait_ge(T.sem["sent"], sent[0])
+    for s in ("dr", "dx", "dc", "oy0", "oy1", "oc"):
+        g.sync.wait_ge(T.sem[s], 16)

@@ -6,13 +6,13 @@ n = 256 // NC
 NL = n // 16
 ROUNDS = 5
 CW = 1408
-MODE1 = "MAMA"
-MODE2 = "MAMA"
+MODE1 = "AMMM"
+MODE2 = "AMAM"
 HG = 2
 
 SCRATCH = {
     "xw": ("sbuf", [128, 2560], "bfloat16"), "ri": ("sbuf", [128, 256], "int32"), "ci": ("sbuf", [128, 1024], "int32"),
-    "cc": ("sbuf", [128, CW], "float32"), "cy": ("sbuf", [128, CW], "float32"), "iot": ("sbuf", [128, 1024], "float32"),
+    "cc": ("sbuf", [128, CW], "float32"), "cy": ("sbuf", [128, CW], "float32"),
     "rf": ("sbuf", [128, 256 * ROUNDS], "float16"), "sd": ("sbuf", [128, 256 * ROUNDS], "float16"),
     "rl": ("sbuf", [128, 512], "uint16"), "rls": ("sbuf", [128, 512], "uint16"),
     "rl2": ("sbuf", [128, 512], "uint16"), "rls2": ("sbuf", [128, 512], "uint16"),
@@ -28,16 +28,14 @@ SCRATCH = {
     "t5": ("sbuf", [128, 512], "float32"), "yo": ("sbuf", [128, 256], "float32"),
     "rr": ("sbuf", [128, 16 * ROUNDS], "float32"), "q15": ("sbuf", [128, 256], "float16"),
     "w": ("sbuf", [128, 32], "float32"), "hi": ("sbuf", [128, 32], "int32"), "hj": ("sbuf", [128, 32], "int32"),
-    "hl": ("sbuf", [128, 32], "uint16"), "nf": ("sbuf", [128, 32], "float32"), "hf": ("sbuf", [128, 32], "float32"),
-    "hr": ("sbuf", [128, 512], "float16"), "EQ": ("sbuf", [128, 16, 256], "float16"), "TRI": ("sbuf", [128, 16, 16], "float16"),
-    "lz": ("sbuf", [128, 256], "float16"), "lx": ("sbuf", [128, 16], "float32"), "lo": ("sbuf", [128, 16], "float32"),
-    "tj": ("sbuf", [128, 16], "float32"), "th": ("sbuf", [128, 16], "float32"), "tm": ("sbuf", [128, 16], "float32"),
-    "ts": ("sbuf", [128, 16], "float32"), "off": ("sbuf", [128, 32], "uint16"),
+    "hl": ("sbuf", [128, 32], "uint16"), "nf": ("sbuf", [128, 32], "float32"), "hf": ("sbuf", [128, 32], "float16"),
+    "e3": ("sbuf", [128, 128], "float16"), "lo": ("sbuf", [128, 16], "float32"), "tj": ("sbuf", [128, 16], "float32"),
+    "tm": ("sbuf", [128, 16], "float32"), "ts": ("sbuf", [128, 16], "float32"), "off": ("sbuf", [128, 64], "uint16"),
     "kc": ("sbuf", [128, ROUNDS], "float32"), "kj": ("sbuf", [128, 64], "float32"),
     "col": ("sbuf", [128, 8], "float32"), "one": ("sbuf", [128, 128], "bfloat16"),
     "B8": ("sbuf", [128, 1024], "bfloat16"), "UP": ("sbuf", [128, 1024], "bfloat16"), "UC": ("sbuf", [128, 1024], "bfloat16"),
-    "DD": ("sbuf", [128, 1024], "bfloat16"), "MM": ("sbuf", [128, 1024], "bfloat16"),
-    "W2": ("sbuf", [128, 2048], "bfloat16"), "NW": ("sbuf", [128, 2048], "bfloat16"), "Q": ("sbuf", [128, 16], "bfloat16"),
+    "DD": ("sbuf", [128, 1024], "bfloat16"), "MM": ("sbuf", [128, 1024], "bfloat16"), "MH": ("sbuf", [128, 1024], "bfloat16"),
+    "W2": ("sbuf", [128, 2048], "bfloat16"), "NW": ("sbuf", [128, 2048], "bfloat16"),
 }
 for _k in ("B", "B0", "I", "L", "SH", "SD", "LI", "UI", "US", "LP", "ZN", "ZA", "ZT", "IT", "IK", "I2", "I16", "NI", "NH", "YA",
            "DS", "R15", "C2", "C19"):
@@ -48,7 +46,15 @@ SEMAPHORES = ["v", "s", "p", "q", "sent", "ar", "dr", "dx", "dc", "oy0", "oy1", 
     ["a%d_%d" % (t, c) for t in range(1, ROUNDS) for c in range(NC)]
 WIDE = set(k for k in SCRATCH if SCRATCH[k][2] in ("float32", "int32"))
 
-CY, PE, GA, WAKE, OWN, NET = 0.001, 0.0005, 1.5, 0.12, 0.06, 3.0
+CY, PE, GA, WAKE, OWN, NET = 0.001, 0.0005, 1.6, 0.16, 0.06, 4.0
+TUNE = {
+    'rl': '4341', 'b3': '844484644438', 'rls': '48', 'v1': '87456300', 'm1': '5250527', 'b5': '454860575157', 'b2': '808444432',
+    'f': '23', 'q': '48', 'w': '56', 'hi': '43', 'hj': '56', 'hl': '52', 'nf': '45', 'mk': '72', 'rn': '43', 'cm': '46',
+    'rl2': '4818', 'r2': '8845', 'b1': '4814654663', 'b4': '34347541', 'b6': '4414843', 'b7': '1254548', 'b0': '76842336',
+    'em': '3321', 'rls2': '7', 'v2': '0200455', 'm2': '231700', 'ad': '112', 'hd': '443', 'qd': '7742', 'g1': '663', 'eq': '512',
+    'ins': '68', 't3': '8845', 'r3': '5682', 'fs': '4418', 'fz': '445', 'nr': '4481', 't4': '4608', 'sd': '4846', 'send': '867',
+    'r3c': '3432', 'q5': '341', 'k5': '0446', 't5': '846', 'e3': '5', 'lo': '3', 'cc': '5276642224604340', 'yo': '0447',
+    'dma': '226', 'cy': '36312546568454123'}
 
 
 def R(name, a, b, step=1):
@@ -57,7 +63,7 @@ def R(name, a, b, step=1):
 
 def size(r):
     s = r[3][-1]
-    return 256 if len(r) > 4 else len(range(s.start, s.stop, s.step or 1))
+    return len(range(s.start, s.stop, s.step or 1))
 
 
 def ind(win, off):
@@ -72,7 +78,7 @@ def make_plan():
     ops = []
 
     def op(queue, kind, args, reads, writes, cost, **kw):
-        d = dict(i=len(ops), q=queue, kind=kind, args=args, r=[], w=list(writes), cost=cost, sem=None)
+        d = dict(i=len(ops), q=queue, kind=kind, args=args, r=[], w=list(writes), cost=cost, sem=None, pb=0)
         for x in reads:
             if isref(x):
                 d["r"] += [x[1], x[2]] if x[0] == "ind" else [x]
@@ -99,8 +105,7 @@ def make_plan():
         return op("v", "tt", (out, in0, in1, o), [in0, in1], [out], c)
 
     def cp(out, in_):
-        k = size(out)
-        return op("v", "cp", (out, in_), [in_], [out], 0.05 + k * GA * CY if in_[0] == "ind" else max(64, k) * CY)
+        return op("v", "cp", (out, in_), [in_], [out], max(64, size(out)) * CY)
 
     def ms(out, val):
         return op("v", "ms", (out, val), [], [out], max(64, size(out) * (.5 if two(out) else 1)) * CY)
@@ -123,9 +128,6 @@ def make_plan():
             rd += [m[1], m[2]]
         return op("p", "mm", mms, rd, sorted(set((m[0][0], m[0][1], m[0][2]) for m in mms)), sum(max(64, size(m[2])) for m in mms) * PE)
 
-    def iota(out, pat, base, cm):
-        return op("q", "iota", (out, pat, base, cm), [K("SH")], [out], 0.13 + 2 * size(out) * CY)
-
     def sel(out, in_, pat, cmp, fill, base, cm):
         return op("q", "sel", (out, in_, pat, cmp, fill, base, cm), [in_], [out], 0.17 + 2 * size(out) * CY)
 
@@ -134,7 +136,7 @@ def make_plan():
 
     dma("dr", R("ri", 0, 256), ("T", "r0"), [], [R("ri", 0, 256)], 2.2)
     dma("dx", R("xw", 0, 2560), ("T", "x"), [], [R("xw", 0, 2560)], 5.0)
-    dma("dc", R("ci", 0, 1024), ("T", "c0"), [], [R("ci", 0, 1024)], 7.5)
+    dma("dc", R("ci", 0, 1024), ("T", "c0"), [R("xw", 0, 2560)], [R("ci", 0, 1024)], 4.5)
     IN = [[-16, 8], [-1, 16]]
     boost(1000, ms(K("one"), 1.0))
     sel(K("B0"), K("one"), [[-16, 8], [0, 16]], A.is_ge, 0.0, 0, 1)
@@ -199,6 +201,11 @@ def make_plan():
         o = "b%d" % (6 + h)
         mm(*sum([grp(T1(o, i), (T1("UP", 4 * h + i), T1("UP", 4 * h + i)), ("I", T1("UC", 4 * h + i))) for i in range(4)], []))
         act(R("MM", 512 * h, 512 * h + 512), R(o, 0, 512), F.Copy)
+    for h in range(2):
+        o = "b%d" % (6 + h)
+        mm(*sum([grp(T1(o, i), (T1("UP", 4 * h + i), K("I")), ("I", T1("UC", 4 * h + i)), ("I", K("I")), ("NI", T1("MM", 4 * h + i)))
+                 for i in range(4)], []))
+        act(R("MH", 512 * h, 512 * h + 512), R(o, 0, 512), F.Copy)
     tt(K("LI"), K("L"), K("I"), A.add)
     tt(K("UI"), K("B"), K("L"), A.subtract)
     tt(K("US"), K("B"), K("LI"), A.subtract)
@@ -207,12 +214,13 @@ def make_plan():
     tt(K("YA"), K("I"), K("SD"), A.add)
     tt(K("DS"), K("SD"), K("I"), A.subtract)
     ts(K("R15"), K("one"), R("col", 0, 1), None, A.mult)
-    iota(R("iot", 0, 1024), [[1, 1024]], 0, 0)
-    iota(R("tj", 0, 16), [[16, 16]], 1024, 1)
+    op("q", "iota", (R("tj", 0, 16), [[16, 16]], 1024, 1), [K("SH")], [R("tj", 0, 16)], 0.17)
 
     X = R("xw", 0, 2560)
     sends = {}
+    starts = []
     for t in range(ROUNDS):
+        starts.append(len(ops))
         P2 = 256 * (t % 2)
         last = t == ROUNDS - 1
 
@@ -223,10 +231,7 @@ def make_plan():
         def b(c, i, k=n):
             return R("b%d" % c, 64 * i, 64 * i + k)
 
-        def lw(name, c):
-            return R(name, 16 * (t % 2) + NL * c, 16 * (t % 2) + NL * c + NL)
-
-        def distances(c, rin, rl, rls, vb, mb, tile, mode):
+        def distances(c, rin, rl, rls, vb, mb, out, mode):
             v0 = 1024 * c
             if mode == "M":
                 mm(*grp(b(c, 0), ("SH", rin)))
@@ -237,53 +242,57 @@ def make_plan():
                 act(vh, ind(X, R(rl[0], rl[1] + u, rl[1] + z)), F.Copy)
                 if mode == "M":
                     tt(R(mb, v0 + w * h, v0 + w * h + w), ind(X, R(rls[0], rls[1] + u, rls[1] + z)), vh, A.max)
-            red = [(R("W2", 128 * p, 128 * p + 128), R(mb, v0 + p, v0 + 1024, 16)) for p in range(15)]
+            red = [(T1("W2", p), R(mb, v0 + p, v0 + 1024, 16)) for p in range(15)]
             if mode == "M":
-                red += [(R("NW", 128 * p, 128 * p + 128), R(vb, v0 + p, v0 + 1024, 16)) for p in range(16)]
-            else:
-                for h in range(2):
-                    e = "b%d" % (6 + (c + h) % 2)
-                    a = v0 + 512 * h
-                    mm(*grp(R(e, 0, 511), ("I", R(vb, a + 1, a + 512)), ("NI", R(vb, a, a + 511))))
-                    act(R(mb, a, a + 511), R(e, 0, 511), F.Abs, scale=0.5)
-            return grp(R("b%d" % (4 + c % 2), 64 * tile, 64 * tile + n), *red)
+                o = grp(out, *([(T1("NW", p), R(vb, v0 + p, v0 + 1024, 16)) for p in range(16)] + red))
+                mm(*o[:16])
+                return o[16:]
+            for h in range(2):
+                e = "b%d" % (6 + (c + h) % 2)
+                a = v0 + 512 * h
+                mm(*grp(R(e, 0, 511), ("I", R(vb, a + 1, a + 512)), ("NI", R(vb, a, a + 511))))
+                act(R(mb, a, a + 511), R(e, 0, 511), F.Abs, scale=0.5)
+            return grp(out, *red)
 
-        for c in range(NC):
+        for c in range(NC - 1, -1, -1):
             rin = R("rf", 256 * t + n * c, 256 * t + n * c + n)
             if t:
                 op("n", "arr", (), [], [rin], 0.0, sem="a%d_%d" % (t, c), tdep=(sends[t - 1, c], NET))
             ts(G("rl", c), rin, 1280.0)
-            mm(*distances(c, rin, G("rl", c), G("rls", c), "v1", "m1", 0, MODE1[c]))
-            ts(G("f", c), R("b%d" % (4 + c % 2), 0, n), 34.5, None, A.is_gt)
-            mm(*(grp(b(c, 1), ("I", rin), ("ZA", G("f", c))) + grp(b(c, 2), ("I", rin), ("ZN", G("f", c)))))
-            ts(G("q", c), b(c, 1), 6911.0, -8191.0, A.max, A.add)
-            q0 = G("q", c)[1]
-            mm(*grp(b(c, 3, NL), ("C2", R("one", 0, NL)),
-                    *[(R("W2", 128 * j, 128 * j + 128), R("q", q0 + j, q0 + n, 16)) for j in range(16)]))
-            tt(lw("w", c), b(c, 3, NL), R("rr", 16 * t + NL * c, 16 * t + NL * c + NL), A.mult)
-            ts(lw("hi", c), lw("w", c), R("kc", t, t + 1))
-            ts(lw("hj", c), lw("hi", c), 1023, None, A.bitwise_and)
-            cp(lw("hl", c), lw("hj", c))
-            ts(lw("nf", c), b(c, 3, NL), -1.0, -4096.0, A.is_lt, A.mult)
-            ts(G("mk", c), b(c, 1), -1280.5, None, A.is_lt)
-            ts(G("rn", c), b(c, 2), -1280.0, None, A.max)
-            tt(G("cm", c), ind(R("cc", 0, 1024), lw("hl", c)), G("mk", c), A.mult)
-            mm(*grp(b(c, 4), ("I", G("rn", c)), ("IK", G("mk", c)), ("IT", G("cm", c))))
-            ts(G("rl2", c), b(c, 4), 1280.0)
-            ts(G("r2", c), b(c, 4), 0.0)
-        if t == 0:
-            ms(R("Q", 0, 16), 0.0)
-            for e in range(8):
-                sel(R("Q", 0, 16), R("Q", 0, 16), [[-1, 16]], A.not_equal, 1.0, -16 * e, 1)
-            mm(*grp(R("b4", 288, 304), ("US", R("Q", 0, 16))))
-            for j in range(16):
-                act(("TRI", 16 * j, 16 * j + 16, (slice(None), j, slice(0, 16))), R("b4", 288, 304), F.Copy)
-        for c in range(NC):
+            D = R("b%d" % (4 + c // 2), n * (c % 2), n * (c % 2) + n)
+            mm(*distances(c, rin, G("rl", c), G("rls", c), "v1", "m1", D, MODE1[c]))
+            if c % 2:
+                continue
+            m, d = 2 * n, c // 2
+            rin = R("rf", 256 * t + m * d, 256 * t + m * d + m)
+            g2 = lambda nm: R(nm, P2 + m * d, P2 + m * d + m)
+            l2 = lambda nm: R(nm, 16 * (t % 2) + 2 * NL * d, 16 * (t % 2) + 2 * NL * d + 2 * NL)
+            e = "b%d" % (c + 1)
+            Z1, Z2, Y2 = R(e, 128, 256), R(e, 384, 512), R(e, 0, 2 * NL)
+            ts(g2("f"), R("b%d" % (4 + d), 0, m), 34.5, None, A.is_gt)
+            mm(*(grp(Z1, ("I", rin), ("ZA", g2("f"))) + grp(Z2, ("I", rin), ("ZN", g2("f")))))
+            ts(g2("q"), Z1, 6911.0, -8191.0, A.max, A.add)
+            q0 = g2("q")[1]
+            mm(*grp(Y2, ("C2", R("one", 0, 2 * NL)), *[(T1("W2", j), R("q", q0 + j, q0 + m, 16)) for j in range(16)]))
+            tt(l2("w"), Y2, R("rr", 16 * t + 2 * NL * d, 16 * t + 2 * NL * d + 2 * NL), A.mult)
+            ts(l2("hi"), l2("w"), R("kc", t, t + 1))
+            ts(l2("hj"), l2("hi"), 1023, None, A.bitwise_and)
+            cp(l2("hl"), l2("hj"))
+            ts(l2("nf"), Y2, -1.0, -4096.0, A.is_lt, A.mult)
+            ts(g2("mk"), Z1, -1280.5, None, A.is_lt)
+            ts(g2("rn"), Z2, -1280.0, None, A.max)
+            tt(g2("cm"), ind(R("cc", 0, 1024), l2("hl")), g2("mk"), A.mult)
+            for i in (c + 1, c):
+                mm(*grp(b(i, 4), ("I", G("rn", i)), ("IK", G("mk", i)), ("IT", G("cm", i))))
+                ts(G("rl2", i), b(i, 4), 1280.0)
+                ts(G("r2", i), b(i, 4), 0.0)
+        for c in range(NC - 1, -1, -1):
             e = "b%d" % (6 + c % 2)
             mm(*sum([grp(R(e, n * s, n * s + n), (T1("DD", s), G("r2", c))) for s in range(8)], []))
-            em = R("em", 2 * 1024 * (t % 2) + 512 * c, 2 * 1024 * (t % 2) + 512 * c + 512)
+            em = R("em", 2048 * (t % 2) + 512 * c, 2048 * (t % 2) + 512 * c + 512)
             ts(em, R(e, 0, 512), 0.0, None, A.is_equal)
-            D1 = distances(c, G("r2", c), G("rl2", c), G("rls2", c), "v2", "m2", 1, MODE2[c])
+            D = "b%d" % (4 + c % 2)
+            D1 = distances(c, G("r2", c), G("rl2", c), G("rls2", c), "v2", "m2", R(D, 128, 128 + n), MODE2[c])
             v0 = 1024 * c
             mm(*grp(R(e, 0, 511), ("I", R("v2", v0 + 2, v0 + 1024, 2)), ("NI", R("v2", v0, v0 + 1022, 2))))
             act(R("ad", 512 * c, 512 * c + 511), R(e, 0, 511), F.Abs, scale=0.5)
@@ -299,10 +308,9 @@ def make_plan():
             tt(G("t3", c), b(c, 0), G("ins", c), A.mult)
             tt(G("r3", c), b(c, 4), G("t3", c), A.add)
             mm(*D1)
-            D = "b%d" % (4 + c % 2)
-            mm(*grp(R(D, 128, 128 + n), *[(T1("W2", p + 1), R("ad", 512 * c + p // 2, 512 * c + 512, 8)) for p in range(0, 13, 2)]))
+            mm(*grp(R(D, 192, 192 + n), *[(T1("W2", p + 1), R("ad", 512 * c + p // 2, 512 * c + 512, 8)) for p in range(0, 13, 2)]))
             fs, fz = G("fs", c, 2 * n), G("fz", c, 2 * n)
-            ts(fs, R(D, 64, 64 + 2 * n), 34.5, 64.5, A.is_gt, A.mult)
+            ts(fs, R(D, 128, 128 + 2 * n), 34.5, 64.5, A.is_gt, A.mult)
             tt(fz, fs, R("b%d" % c, 64, 64 + 2 * n), A.is_gt)
             f2, F2 = R("fz", fz[1], fz[1] + n), R("fz", fz[1] + n, fz[1] + 2 * n)
             mm(*(grp(b(c, 5), ("I2", G("ins", c)), ("YA", f2), ("I16", F2)) + grp(b(c, 6), ("DS", G("r3", c)))))
@@ -315,43 +323,44 @@ def make_plan():
             act(G("r3c", c), G("r3", c), F.Identity if last else F.Copy, bias=1280.0 if last else 0.0)
             if last:
                 tt(R("yo", n * c, n * c + n), G("r3c", c), G("t4", c), A.add)
-                if c % 2:
-                    x = n * (c - 1)
+                if c % 2 == 0:
+                    x = n * c
                     dma("oy%d" % (c // 2), ("T", "yr", x, x + 2 * n), R("yo", x, x + 2 * n), [R("yo", x, x + 2 * n)], [], 2.0)
             mm(*(grp(b(c, 7), ("I", G("r3", c)), ("ZA", f2)) + grp(b(c, 3), ("LP", f2))))
             ts(G("q5", c), b(c, 7), 6911.0, -8191.0, A.max, A.add)
             act(G("k5", c), b(c, 3), F.Sign)
             mm(*grp(b(c, 0), ("C19", R("one", 0, n)), ("NI", G("r3", c)), ("B", G("q5", c))))
             tt(G("t5", c), b(c, 0), G("k5", c), A.mult)
-            if c == 1:
+            if c == 2:
                 if not last:
                     mm(*grp(R("b5", 320, 384), *[("R15", G("mk", i)) for i in range(NC)]))
                     act(R("kj", 0, 64), R("b5", 320, 384), F.Identity, bias=-0.4921875 / 64, acc=R("kc", t + 1, t + 2))
                 x = 16 * (t % 2)
                 H = lambda nm: R(nm, x, x + 16)
-                act(R("hr", 16 * x, 16 * x + 256), ind(R("iot", 0, 1024), H("hl")), F.Copy)
                 tt(H("hf"), H("hj"), H("nf"), A.add)
-                for j in range(16):
-                    z = 256 - 16 * j
-                    ts(("EQ", 256 * j, 256 * j + z, (slice(None), j, slice(0, z))), R("hr", 16 * x + 16 * j, 16 * x + 256),
-                       R("hf", x + j, x + j + 1), None, A.is_equal)
-                dg = ("EQ", 0, 4096, (slice(None), slice(0, 16), slice(0, 16)), 3)
-                tt(dg, dg, ("TRI", 0, 256, (slice(None), slice(0, 16), slice(0, 16)), 3), A.mult)
-                mm(*[(R("b4", 256 + 16 * j, 512), K("B"), ("EQ", 256 * j, 512 * j + 256 - 16 * j - 256 * j, (slice(None), j, slice(0, 256 - 16 * j))),
-                      j == 0, j == 15) for j in range(16)])
-                act(R("lz", 0, 256), R("b4", 256, 512), F.Sign)
-                mm(*grp(R("b5", 256, 272), *[(R("W2", 128 * j, 128 * j + 128), R("lz", j, 256, 16)) for j in range(16)]))
-                tt(R("lx", 0, 16), R("b5", 256, 272), H("nf"), A.subtract)
-                ts(R("lo", 0, 16), R("lx", 0, 16), 1.0, None, A.is_ge)
-                tt(R("th", 0, 16), R("tj", 0, 16), H("hj"), A.subtract)
-                tt(R("tm", 0, 16), R("lo", 0, 16), R("th", 0, 16), A.mult)
-                tt(R("ts", 0, 16), R("tm", 0, 16), H("hj"), A.add)
-                cp(H("off"), R("ts", 0, 16))
+                mm(*sum([grp(R("b4", 256 + 16 * e, 272 + 16 * e), (T1("DD", e), H("hf"))) for e in range(8)], []))
+                ts(R("e3", 0, 128), R("b4", 256, 384), 0.0, None, A.is_equal)
+                mm(*grp(R("b5", 256, 272), *[(T1("MH", e), R("e3", 16 * e, 16 * e + 16)) for e in range(8)]))
+                tt(R("lo", 0, 16), R("b5", 256, 272), H("nf"), A.is_gt)
+                tt(R("tm", 0, 16), R("lo", 0, 16), R("tj", 0, 16), A.mult)
+                tt(R("ts", 0, 16), H("hj"), R("tm", 0, 16), A.max)
+                cp(R("off", 2 * x, 2 * x + 32, 2), R("ts", 0, 16))
                 if last:
                     act(R("cy", 0, 1024), R("cc", 0, 1024), F.Identity, bias=1280.0)
-        for c in range(NC):
-            tt(ind(R("cy" if last else "cc", 0, CW), lw("off", c)), G("t5", c), G("r3c", c), A.add)
+        for j in range(15, -1, -1):
+            a = P2 + 16 * j
+            tt(ind(R("cy" if last else "cc", 0, CW), R("off", 32 * (t % 2) + 2 * j, 32 * (t % 2) + 2 * j + 1)),
+               R("t5", a, a + 16), R("r3c", a, a + 16), A.add)
     dma("oc", ("T", "yc", 0, 1024), R("cy", 0, 1024), [R("cy", 0, 1024)], [], 4.0)
+    for t in range(ROUNDS):
+        cnt = {}
+        for o in ops[starts[t]:(starts + [len(ops)])[t + 1]]:
+            if o["kind"] != "arr":
+                nm = o["w"][0][0] if o["w"] else o["kind"]
+                k = cnt.get(nm, 0)
+                cnt[nm] = k + 1
+                s = TUNE.get(nm, "")
+                o["pb"] += int(s[k]) - 4 if k < len(s) else 0
     return ops
 
 
@@ -364,7 +373,7 @@ def link(ops):
             name, a, b = r[0], r[1], r[2]
             ps = SCRATCH[name][0] == "psum"
             for (x, y, pw, po) in seen.get(name, ()):
-                if po is not o and ((a < y and x < b and (wr or pw)) or (ps and po["q"] != o["q"])):
+                if po is not o and ((a < y and x < b and (wr or pw)) or (ps and (po["q"] != o["q"] or name in ("b4", "b5")))):
                     dep.add(po["i"])
         for r, wr in acc:
             name, a, b = r[0], r[1], r[2]
@@ -388,7 +397,7 @@ def schedule(ops):
     pri = [0.0] * N
     for i in range(N - 1, -1, -1):
         pri[i] = ops[i]["cost"] + max([lat + pri[j] for j, lat in succ[i]] + [0.0])
-    pri = [x + o.get("pb", 0) for x, o in zip(pri, ops)]
+    pri = [x + o["pb"] for x, o in zip(pri, ops)]
     est = [0.0] * N
     ready = {}
     for o in ops:

from concourse.bass import DstId, RemoteDMATransfer
from concourse.mybir import dt, AluOpType as A, AxisListType, ActivationFunctionType as F

NC = 4
n = 256 // NC
NL = n // 16
ROUNDS = 5
CW = 1408
MODE1 = "AMMM"
MODE2 = "AMAM"
HG = 2

SCRATCH = {
    "xw": ("sbuf", [128, 2560], "bfloat16"), "ri": ("sbuf", [128, 256], "int32"), "ci": ("sbuf", [128, 1024], "int32"),
    "cc": ("sbuf", [128, CW], "float32"), "cy": ("sbuf", [128, CW], "float32"),
    "rf": ("sbuf", [128, 256 * ROUNDS], "float16"), "sd": ("sbuf", [128, 256 * ROUNDS], "float16"),
    "rl": ("sbuf", [128, 512], "uint16"), "rls": ("sbuf", [128, 512], "uint16"),
    "rl2": ("sbuf", [128, 512], "uint16"), "rls2": ("sbuf", [128, 512], "uint16"),
    "v1": ("sbuf", [128, 4096], "bfloat16"), "m1": ("sbuf", [128, 4096], "bfloat16"),
    "v2": ("sbuf", [128, 4096], "bfloat16"), "m2": ("sbuf", [128, 4096], "bfloat16"), "ad": ("sbuf", [128, 2048], "bfloat16"),
    "f": ("sbuf", [128, 512], "float16"), "q": ("sbuf", [128, 512], "float16"), "mk": ("sbuf", [128, 512], "float16"),
    "rn": ("sbuf", [128, 512], "float16"), "cm": ("sbuf", [128, 512], "float16"), "r2": ("sbuf", [128, 512], "float16"),
    "em": ("sbuf", [128, 4096], "float16"), "hd": ("sbuf", [128, 512], "float16"), "g1": ("sbuf", [128, 512], "float16"),
    "qd": ("sbuf", [128, 512], "float16"), "eq": ("sbuf", [128, 512], "float16"), "ins": ("sbuf", [128, 512], "float16"),
    "t3": ("sbuf", [128, 512], "float32"), "r3": ("sbuf", [128, 512], "float16"), "r3c": ("sbuf", [128, 512], "float32"),
    "fs": ("sbuf", [128, 1024], "float16"), "fz": ("sbuf", [128, 1024], "float16"), "nr": ("sbuf", [128, 512], "float16"),
    "t4": ("sbuf", [128, 512], "float32"), "q5": ("sbuf", [128, 512], "float16"), "k5": ("sbuf", [128, 512], "float16"),
    "t5": ("sbuf", [128, 512], "float32"), "yo": ("sbuf", [128, 256], "float32"),
    "rr": ("sbuf", [128, 16 * ROUNDS], "float32"), "q15": ("sbuf", [128, 256], "float16"),
    "w": ("sbuf", [128, 32], "float32"), "hi": ("sbuf", [128, 32], "int32"), "hj": ("sbuf", [128, 32], "int32"),
    "hl": ("sbuf", [128, 32], "uint16"), "nf": ("sbuf", [128, 32], "float32"), "hf": ("sbuf", [128, 32], "float16"),
    "e3": ("sbuf", [128, 128], "float16"), "lo": ("sbuf", [128, 16], "float32"), "tj": ("sbuf", [128, 16], "float32"),
    "tm": ("sbuf", [128, 16], "float32"), "ts": ("sbuf", [128, 16], "float32"), "off": ("sbuf", [128, 64], "uint16"),
    "kc": ("sbuf", [128, ROUNDS], "float32"), "kj": ("sbuf", [128, 64], "float32"),
    "col": ("sbuf", [128, 8], "float32"), "one": ("sbuf", [128, 128], "bfloat16"),
    "B8": ("sbuf", [128, 1024], "bfloat16"), "UP": ("sbuf", [128, 1024], "bfloat16"), "UC": ("sbuf", [128, 1024], "bfloat16"),
    "DD": ("sbuf", [128, 1024], "bfloat16"), "MM": ("sbuf", [128, 1024], "bfloat16"), "MH": ("sbuf", [128, 1024], "bfloat16"),
    "W2": ("sbuf", [128, 2048], "bfloat16"), "NW": ("sbuf", [128, 2048], "bfloat16"),
}
for _k in ("B", "B0", "I", "L", "SH", "SD", "LI", "UI", "US", "LP", "ZN", "ZA", "ZT", "IT", "IK", "I2", "I16", "NI", "NH", "YA",
           "DS", "R15", "C2", "C19"):
    SCRATCH[_k] = ("sbuf", [128, 128], "bfloat16")
for _k in range(8):
    SCRATCH["b%d" % _k] = ("psum", [128, 512], "float32")
SEMAPHORES = ["v", "s", "p", "q", "sent", "ar", "dr", "dx", "dc", "oy0", "oy1", "oc"] + \
    ["a%d_%d" % (t, c) for t in range(1, ROUNDS) for c in range(NC)]
WIDE = set(k for k in SCRATCH if SCRATCH[k][2] in ("float32", "int32"))

CY, PE, GA, WAKE, OWN, NET = 0.001, 0.0005, 1.6, 0.16, 0.06, 4.0
TUNE = {
    'rl': '4341', 'b3': '844484644438', 'rls': '48', 'v1': '87456300', 'm1': '5250527', 'b5': '454860575157', 'b2': '808444432',
    'f': '23', 'q': '48', 'w': '56', 'hi': '43', 'hj': '56', 'hl': '52', 'nf': '45', 'mk': '72', 'rn': '43', 'cm': '46',
    'rl2': '4818', 'r2': '8845', 'b1': '4814654663', 'b4': '34347541', 'b6': '4414843', 'b7': '1254548', 'b0': '76842336',
    'em': '3321', 'rls2': '7', 'v2': '0200455', 'm2': '231700', 'ad': '112', 'hd': '443', 'qd': '7742', 'g1': '663', 'eq': '512',
    'ins': '68', 't3': '8845', 'r3': '5682', 'fs': '4418', 'fz': '445', 'nr': '4481', 't4': '4608', 'sd': '4846', 'send': '867',
    'r3c': '3432', 'q5': '341', 'k5': '0446', 't5': '846', 'e3': '5', 'lo': '3', 'cc': '5276642224604340', 'yo': '0447',
    'dma': '226', 'cy': '36312546568454123'}


def R(name, a, b, step=1):
    return (name, a, b, (slice(None), slice(a, b, step)))


def size(r):
    s = r[3][-1]
    return len(range(s.start, s.stop, s.step or 1))


def ind(win, off):
    return ("ind", win, off)


def isref(x):
    return isinstance(x, tuple)


def make_plan():
    ops = []

    def op(queue, kind, args, reads, writes, cost, **kw):
        d = dict(i=len(ops), q=queue, kind=kind, args=args, r=[], w=list(writes), cost=cost, sem=None, pb=0)
        for x in reads:
            if isref(x):
                d["r"] += [x[1], x[2]] if x[0] == "ind" else [x]
        d.update(kw)
        ops.append(d)
        return d

    def boost(x, o):
        o["pb"] = x

    two = lambda r: r[0] not in WIDE and r[0][0] != "b"

    def ts(out, in0, s1, s2=None, op0=A.add, op1=None):
        c = max(64, size(in0) * (0.5 if two(out) and two(in0) else 1)) * CY
        return op("v", "ts", (out, in0, s1, s2, op0, op1), [in0, s1, s2], [out], c)

    def tt(out, in0, in1, o):
        if out[0] == "ind":
            return op("v", "tt", (out, in0, in1, o), [in0, in1, out[2]], [out[1]], 0.05 + size(in0) * 3 * CY)
        if in0[0] == "ind":
            c = 0.05 + size(in1) * GA * CY
        else:
            c = max(64, size(in0) * (1 if in0[0][0] == "b" or in1[0][0] == "b" else 2)) * CY
        return op("v", "tt", (out, in0, in1, o), [in0, in1], [out], c)

    def cp(out, in_):
        return op("v", "cp", (out, in_), [in_], [out], max(64, size(out)) * CY)

    def ms(out, val):
        return op("v", "ms", (out, val), [], [out], max(64, size(out) * (.5 if two(out) else 1)) * CY)

    def act(out, in_, fn, bias=0.0, scale=1.0, acc=None):
        k = size(out)
        return op("s", "act", (out, in_, fn, bias, scale, acc), [in_], [out] + ([acc] if acc else []),
                  (0.065 + k * GA * CY) if in_[0] == "ind" else max(64, k) * CY)

    def K(name):
        return R(name, 0, 128)

    def grp(out, *pairs):
        last = len(pairs) - 1
        return [(out, K(a) if isinstance(a, str) else a, b, i == 0, i == last) for i, (a, b) in enumerate(pairs)]

    def mm(*mms):
        rd = []
        for m in mms:
            rd += [m[1], m[2]]
        return op("p", "mm", mms, rd, sorted(set((m[0][0], m[0][1], m[0][2]) for m in mms)), sum(max(64, size(m[2])) for m in mms) * PE)

    def sel(out, in_, pat, cmp, fill, base, cm):
        return op("q", "sel", (out, in_, pat, cmp, fill, base, cm), [in_], [out], 0.17 + 2 * size(out) * CY)

    def dma(sem, out, in_, reads, writes, cost):
        return op("y", "dma", (out, in_), reads, writes, cost, sem=sem)

    dma("dr", R("ri", 0, 256), ("T", "r0"), [], [R("ri", 0, 256)], 2.2)
    dma("dx", R("xw", 0, 2560), ("T", "x"), [], [R("xw", 0, 2560)], 5.0)
    dma("dc", R("ci", 0, 1024), ("T", "c0"), [R("xw", 0, 2560)], [R("ci", 0, 1024)], 4.5)
    IN = [[-16, 8], [-1, 16]]
    boost(1000, ms(K("one"), 1.0))
    sel(K("B0"), K("one"), [[-16, 8], [0, 16]], A.is_ge, 0.0, 0, 1)
    sel(K("B"), K("B0"), [[16, 8], [0, 16]], A.is_ge, 0.0, 15, -1)
    boost(200, sel(K("I"), K("B"), IN, A.is_equal, 0.0, 0, 1))
    boost(100, sel(K("SH"), K("B"), IN, A.is_equal, 0.0, -1, 1))
    ms(R("W2", 0, 2048), 0.0)
    boost(90, sel(K("L"), K("B"), [[16, 8], [1, 16]], A.is_gt, 0.0, 0, -1))
    sel(K("SD"), K("B"), IN, A.is_equal, 0.0, 1, 1)
    for p in range(16):
        a = 128 * p
        ts(("W2", a, a + 128, (slice(None), slice(a + p, a + 128, 16))), R("B", 0, 128, 16), 2.0, None, A.mult)
    act(K("NI"), K("I"), F.Copy, scale=-1.0)
    act(K("NH"), K("I"), F.Copy, scale=-0.5)
    for i in range(4):
        a = 512 * i
        o = R("b%d" % i, 0, 512)
        if i:
            mm(*grp(o, ("NH", R("W2", a, a + 512)), ("NH", R("W2", a - 128, a + 384))))
        else:
            mm(*(grp(R("b0", 0, 128), ("NH", R("W2", 0, 128))) +
                 grp(R("b0", 128, 512), ("NH", R("W2", 128, 512)), ("NH", R("W2", 0, 384)))))
        act(R("NW", a, a + 512), o, F.Copy)
    for c in range(NC):
        ts(R("rf", c * n, c * n + n), R("ri", c * n, c * n + n), -1280.0)
    op("v", "red", (R("col", 0, 1), R("I", 15, 128, 16)), [R("I", 15, 128, 16)], [R("col", 0, 1)], .07)
    op("v", "red", (R("col", 1, 2), R("I", 1, 128, 2)), [R("I", 1, 128, 2)], [R("col", 1, 2)], .07)
    tt(R("col", 2, 3), R("col", 1, 2), R("col", 0, 1), A.subtract)
    ts(R("col", 3, 4), R("col", 2, 3), 3.5, -1.0, A.mult, A.add)
    ts(R("q15", 0, 256), R("rf", 0, 256), R("col", 0, 1), None, A.mult)
    mm(*grp(R("b4", 256, 272), *[(R("W2", 128 * j, 128 * j + 128), R("q15", j, 256, 16)) for j in range(16)]))
    ts(R("rr", 0, 16), R("b4", 256, 272), 1.0 / 256, 10.5, A.mult, A.add)
    op("q", "rsend", (), [R("rr", 0, 16)], [], 1.5)
    op("n", "arr", (), [], [R("rr", 16, 16 * ROUNDS)], 0.0, sem="ar", tdep=(ops[-1], NET))
    act(K("ZT"), K("L"), F.Copy, scale=-16384.0)
    act(K("ZA"), K("I"), F.Copy, scale=8192.0)
    tt(K("ZA"), K("ZA"), K("ZT"), A.add)
    act(K("LP"), K("L"), F.Copy)
    act(R("LP", 15, 128, 16), R("I", 15, 128, 16), F.Copy, scale=0.0)
    act(K("ZN"), K("LP"), F.Copy, scale=-8192.0)
    act(K("IT"), K("I"), F.Copy)
    act(R("IT", 15, 128, 16), R("I", 15, 128, 16), F.Copy, scale=0.0)
    act(K("IK"), K("IT"), F.Copy, scale=1280.0)
    ms(K("C2"), 320.0)
    ms(("C2", 0, 128, (slice(0, 1), slice(0, 128))), 318.0)
    ms(K("C19"), 150.0)
    ms(("C19", 0, 128, (slice(0, 1), slice(0, 128))), 149.0)
    ms(R("kc", 0, 1), -0.4921875)
    ts(R("cc", 0, 1024), R("ci", 0, 1024), -1280.0)
    ms(R("cc", 1024, CW), 0.0)
    ms(R("cy", 1024, CW), 0.0)
    for h in range(8):
        ts(R("B8", 128 * h, 128 * h + 128), K("B"), 1.0, None, A.mult)
    sel(R("UP", 0, 1024), R("B8", 0, 1024), [[-1, 8], [-16, 8], [-1, 16]], A.is_equal, 0.0, -1, 1)
    sel(R("UC", 0, 1024), R("B8", 0, 1024), [[1, 8], [-16, 8], [-1, 16]], A.is_equal, 0.0, -15, 1)
    T1 = lambda nm, s: R(nm, 128 * s, 128 * s + 128)
    for h in range(2):
        o = "b%d" % (6 + h)
        mm(*sum([grp(T1(o, i), ("I", T1("UP", 4 * h + i)), (T1("UC", 4 * h + i), K("I")), ("NI", K("I"))) for i in range(4)], []))
        act(R("DD", 512 * h, 512 * h + 512), R(o, 0, 512), F.Copy)
    for h in range(2):
        o = "b%d" % (6 + h)
        mm(*sum([grp(T1(o, i), (T1("UP", 4 * h + i), T1("UP", 4 * h + i)), ("I", T1("UC", 4 * h + i))) for i in range(4)], []))
        act(R("MM", 512 * h, 512 * h + 512), R(o, 0, 512), F.Copy)
    for h in range(2):
        o = "b%d" % (6 + h)
        mm(*sum([grp(T1(o, i), (T1("UP", 4 * h + i), K("I")), ("I", T1("UC", 4 * h + i)), ("I", K("I")), ("NI", T1("MM", 4 * h + i)))
                 for i in range(4)], []))
        act(R("MH", 512 * h, 512 * h + 512), R(o, 0, 512), F.Copy)
    tt(K("LI"), K("L"), K("I"), A.add)
    tt(K("UI"), K("B"), K("L"), A.subtract)
    tt(K("US"), K("B"), K("LI"), A.subtract)
    act(K("I2"), K("I"), F.Copy, scale=2.0)
    act(K("I16"), K("I"), F.Copy, scale=16.0)
    tt(K("YA"), K("I"), K("SD"), A.add)
    tt(K("DS"), K("SD"), K("I"), A.subtract)
    ts(K("R15"), K("one"), R("col", 0, 1), None, A.mult)
    op("q", "iota", (R("tj", 0, 16), [[16, 16]], 1024, 1), [K("SH")], [R("tj", 0, 16)], 0.17)

    X = R("xw", 0, 2560)
    sends = {}
    starts = []
    for t in range(ROUNDS):
        starts.append(len(ops))
        P2 = 256 * (t % 2)
        last = t == ROUNDS - 1

        def G(name, c, k=n):
            a = (P2 // 64) * (k * NC // 4) + k * c
            return R(name, a, a + k)

        def b(c, i, k=n):
            return R("b%d" % c, 64 * i, 64 * i + k)

        def distances(c, rin, rl, rls, vb, mb, out, mode):
            v0 = 1024 * c
            if mode == "M":
                mm(*grp(b(c, 0), ("SH", rin)))
                ts(rls, b(c, 0), 1280.0)
            for h in range(HG):
                w = 1024 // HG
                vh, u, z = R(vb, v0 + w * h, v0 + w * h + w), n // HG * h, n // HG * h + n // HG
                act(vh, ind(X, R(rl[0], rl[1] + u, rl[1] + z)), F.Copy)
                if mode == "M":
                    tt(R(mb, v0 + w * h, v0 + w * h + w), ind(X, R(rls[0], rls[1] + u, rls[1] + z)), vh, A.max)
            red = [(T1("W2", p), R(mb, v0 + p, v0 + 1024, 16)) for p in range(15)]
            if mode == "M":
                o = grp(out, *([(T1("NW", p), R(vb, v0 + p, v0 + 1024, 16)) for p in range(16)] + red))
                mm(*o[:16])
                return o[16:]
            for h in range(2):
                e = "b%d" % (6 + (c + h) % 2)
                a = v0 + 512 * h
                mm(*grp(R(e, 0, 511), ("I", R(vb, a + 1, a + 512)), ("NI", R(vb, a, a + 511))))
                act(R(mb, a, a + 511), R(e, 0, 511), F.Abs, scale=0.5)
            return grp(out, *red)

        for c in range(NC - 1, -1, -1):
            rin = R("rf", 256 * t + n * c, 256 * t + n * c + n)
            if t:
                op("n", "arr", (), [], [rin], 0.0, sem="a%d_%d" % (t, c), tdep=(sends[t - 1, c], NET))
            ts(G("rl", c), rin, 1280.0)
            D = R("b%d" % (4 + c // 2), n * (c % 2), n * (c % 2) + n)
            mm(*distances(c, rin, G("rl", c), G("rls", c), "v1", "m1", D, MODE1[c]))
            if c % 2:
                continue
            m, d = 2 * n, c // 2
            rin = R("rf", 256 * t + m * d, 256 * t + m * d + m)
            g2 = lambda nm: R(nm, P2 + m * d, P2 + m * d + m)
            l2 = lambda nm: R(nm, 16 * (t % 2) + 2 * NL * d, 16 * (t % 2) + 2 * NL * d + 2 * NL)
            e = "b%d" % (c + 1)
            Z1, Z2, Y2 = R(e, 128, 256), R(e, 384, 512), R(e, 0, 2 * NL)
            ts(g2("f"), R("b%d" % (4 + d), 0, m), 34.5, None, A.is_gt)
            mm(*(grp(Z1, ("I", rin), ("ZA", g2("f"))) + grp(Z2, ("I", rin), ("ZN", g2("f")))))
            ts(g2("q"), Z1, 6911.0, -8191.0, A.max, A.add)
            q0 = g2("q")[1]
            mm(*grp(Y2, ("C2", R("one", 0, 2 * NL)), *[(T1("W2", j), R("q", q0 + j, q0 + m, 16)) for j in range(16)]))
            tt(l2("w"), Y2, R("rr", 16 * t + 2 * NL * d, 16 * t + 2 * NL * d + 2 * NL), A.mult)
            ts(l2("hi"), l2("w"), R("kc", t, t + 1))
            ts(l2("hj"), l2("hi"), 1023, None, A.bitwise_and)
            cp(l2("hl"), l2("hj"))
            ts(l2("nf"), Y2, -1.0, -4096.0, A.is_lt, A.mult)
            ts(g2("mk"), Z1, -1280.5, None, A.is_lt)
            ts(g2("rn"), Z2, -1280.0, None, A.max)
            tt(g2("cm"), ind(R("cc", 0, 1024), l2("hl")), g2("mk"), A.mult)
            for i in (c + 1, c):
                mm(*grp(b(i, 4), ("I", G("rn", i)), ("IK", G("mk", i)), ("IT", G("cm", i))))
                ts(G("rl2", i), b(i, 4), 1280.0)
                ts(G("r2", i), b(i, 4), 0.0)
        for c in range(NC - 1, -1, -1):
            e = "b%d" % (6 + c % 2)
            mm(*sum([grp(R(e, n * s, n * s + n), (T1("DD", s), G("r2", c))) for s in range(8)], []))
            em = R("em", 2048 * (t % 2) + 512 * c, 2048 * (t % 2) + 512 * c + 512)
            ts(em, R(e, 0, 512), 0.0, None, A.is_equal)
            D = "b%d" % (4 + c % 2)
            D1 = distances(c, G("r2", c), G("rl2", c), G("rls2", c), "v2", "m2", R(D, 128, 128 + n), MODE2[c])
            v0 = 1024 * c
            mm(*grp(R(e, 0, 511), ("I", R("v2", v0 + 2, v0 + 1024, 2)), ("NI", R("v2", v0, v0 + 1022, 2))))
            act(R("ad", 512 * c, 512 * c + 511), R(e, 0, 511), F.Abs, scale=0.5)
            mm(*grp(b(c, 5), *[(T1("MM", s), R("em", em[1] + n * s, em[1] + n * s + n)) for s in range(8)]))
            ts(G("hd", c), b(c, 5), 1.0, None, A.is_ge)
            mm(*grp(b(c, 6), ("I", G("r2", c)), ("ZA", G("hd", c))))
            ts(G("qd", c), b(c, 6), 6911.0, -8191.0, A.max, A.add)
            ts(G("g1", c), b(c, 6), 4000.0, 64.0, A.is_gt, A.mult)
            mm(*grp(b(c, 0), ("C19", R("one", 0, n)), ("NI", G("r2", c)), ("B", G("qd", c))))
            ts(G("eq", c), b(c, 0), 0.0, None, A.is_equal)
            mm(*(grp(b(c, 1), ("LI", G("g1", c)), ("US", G("eq", c))) + grp(b(c, 2), ("LI", G("g1", c)), ("UI", G("eq", c)))))
            ts(G("ins", c), b(c, 2), 64.5, None, A.is_gt)
            tt(G("t3", c), b(c, 0), G("ins", c), A.mult)
            tt(G("r3", c), b(c, 4), G("t3", c), A.add)
            mm(*D1)
            mm(*grp(R(D, 192, 192 + n), *[(T1("W2", p + 1), R("ad", 512 * c + p // 2, 512 * c + 512, 8)) for p in range(0, 13, 2)]))
            fs, fz = G("fs", c, 2 * n), G("fz", c, 2 * n)
            ts(fs, R(D, 128, 128 + 2 * n), 34.5, 64.5, A.is_gt, A.mult)
            tt(fz, fs, R("b%d" % c, 64, 64 + 2 * n), A.is_gt)
            f2, F2 = R("fz", fz[1], fz[1] + n), R("fz", fz[1] + n, fz[1] + 2 * n)
            mm(*(grp(b(c, 5), ("I2", G("ins", c)), ("YA", f2), ("I16", F2)) + grp(b(c, 6), ("DS", G("r3", c)))))
            ts(G("nr", c), b(c, 5), R("col", 3, 4), None, A.is_lt)
            tt(G("t4", c), b(c, 6), G("nr", c), A.mult)
            if not last:
                so = R("sd", 256 * t + n * c, 256 * t + n * c + n)
                tt(so, G("r3", c), G("t4", c), A.add)
                sends[t, c] = op("q", "send", (t, c), [so], [], 1.0)
            act(G("r3c", c), G("r3", c), F.Identity if last else F.Copy, bias=1280.0 if last else 0.0)
            if last:
                tt(R("yo", n * c, n * c + n), G("r3c", c), G("t4", c), A.add)
                if c % 2 == 0:
                    x = n * c
                    dma("oy%d" % (c // 2), ("T", "yr", x, x + 2 * n), R("yo", x, x + 2 * n), [R("yo", x, x + 2 * n)], [], 2.0)
            mm(*(grp(b(c, 7), ("I", G("r3", c)), ("ZA", f2)) + grp(b(c, 3), ("LP", f2))))
            ts(G("q5", c), b(c, 7), 6911.0, -8191.0, A.max, A.add)
            act(G("k5", c), b(c, 3), F.Sign)
            mm(*grp(b(c, 0), ("C19", R("one", 0, n)), ("NI", G("r3", c)), ("B", G("q5", c))))
            tt(G("t5", c), b(c, 0), G("k5", c), A.mult)
            if c == 2:
                if not last:
                    mm(*grp(R("b5", 320, 384), *[("R15", G("mk", i)) for i in range(NC)]))
                    act(R("kj", 0, 64), R("b5", 320, 384), F.Identity, bias=-0.4921875 / 64, acc=R("kc", t + 1, t + 2))
                x = 16 * (t % 2)
                H = lambda nm: R(nm, x, x + 16)
                tt(H("hf"), H("hj"), H("nf"), A.add)
                mm(*sum([grp(R("b4", 256 + 16 * e, 272 + 16 * e), (T1("DD", e), H("hf"))) for e in range(8)], []))
                ts(R("e3", 0, 128), R("b4", 256, 384), 0.0, None, A.is_equal)
                mm(*grp(R("b5", 256, 272), *[(T1("MH", e), R("e3", 16 * e, 16 * e + 16)) for e in range(8)]))
                tt(R("lo", 0, 16), R("b5", 256, 272), H("nf"), A.is_gt)
                tt(R("tm", 0, 16), R("lo", 0, 16), R("tj", 0, 16), A.mult)
                tt(R("ts", 0, 16), H("hj"), R("tm", 0, 16), A.max)
                cp(R("off", 2 * x, 2 * x + 32, 2), R("ts", 0, 16))
                if last:
                    act(R("cy", 0, 1024), R("cc", 0, 1024), F.Identity, bias=1280.0)
        for j in range(15, -1, -1):
            a = P2 + 16 * j
            tt(ind(R("cy" if last else "cc", 0, CW), R("off", 32 * (t % 2) + 2 * j, 32 * (t % 2) + 2 * j + 1)),
               R("t5", a, a + 16), R("r3c", a, a + 16), A.add)
    dma("oc", ("T", "yc", 0, 1024), R("cy", 0, 1024), [R("cy", 0, 1024)], [], 4.0)
    for t in range(ROUNDS):
        cnt = {}
        for o in ops[starts[t]:(starts + [len(ops)])[t + 1]]:
            if o["kind"] != "arr":
                nm = o["w"][0][0] if o["w"] else o["kind"]
                k = cnt.get(nm, 0)
                cnt[nm] = k + 1
                s = TUNE.get(nm, "")
                o["pb"] += int(s[k]) - 4 if k < len(s) else 0
    return ops


def link(ops):
    seen = {}
    for o in ops:
        dep = set()
        acc = [(r, False) for r in o["r"]] + [(w, True) for w in o["w"]]
        for r, wr in acc:
            name, a, b = r[0], r[1], r[2]
            ps = SCRATCH[name][0] == "psum"
            for (x, y, pw, po) in seen.get(name, ()):
                if po is not o and ((a < y and x < b and (wr or pw)) or (ps and (po["q"] != o["q"] or name in ("b4", "b5")))):
                    dep.add(po["i"])
        for r, wr in acc:
            name, a, b = r[0], r[1], r[2]
            keep = [e for e in seen.get(name, ()) if e[3] is o or not (wr and a <= e[0] and e[1] <= b)]
            keep.append((a, b, wr, o))
            seen[name] = keep
        o["dep"] = sorted(dep)


def schedule(ops):
    N = len(ops)
    succ = [[] for _ in range(N)]
    need = [0] * N
    for o in ops:
        for d in o["dep"]:
            succ[d].append((o["i"], OWN if ops[d]["q"] == o["q"] else WAKE))
            need[o["i"]] += 1
        if o.get("tdep"):
            succ[o["tdep"][0]["i"]].append((o["i"], o["tdep"][1]))
            need[o["i"]] += 1
    pri = [0.0] * N
    for i in range(N - 1, -1, -1):
        pri[i] = ops[i]["cost"] + max([lat + pri[j] for j, lat in succ[i]] + [0.0])
    pri = [x + o["pb"] for x, o in zip(pri, ops)]
    est = [0.0] * N
    ready = {}
    for o in ops:
        if not need[o["i"]]:
            ready.setdefault(o["q"], []).append(o["i"])
    free, busy, order = {}, {}, []
    while len(order) < N:
        best = None
        for q, L in ready.items():
            if L:
                f = free.get(q, 0.0)
                s = min(max(f, est[i]) for i in L)
                if best is None or s < best[0]:
                    best = (s, q)
        s, q = best
        f = free.get(q, 0.0)
        i = max([i for i in ready[q] if max(f, est[i]) <= s + 1e-9], key=lambda k: (pri[k], -k))
        ready[q].remove(i)
        o = ops[i]
        o["t0"] = s
        end = s + o["cost"]
        free[q] = s if o["kind"] == "arr" else (s + 0.05 if o["kind"] == "dma" else end)
        busy[q] = busy.get(q, 0.0) + o["cost"]
        order.append(i)
        for j, lat in succ[i]:
            est[j] = max(est[j], end + lat)
            need[j] -= 1
            if not need[j]:
                ready.setdefault(ops[j]["q"], []).append(j)
    return order, max(o["t0"] + o["cost"] for o in ops), busy


def waits(ops, order):
    cnt, know = {}, {}
    for i in order:
        o = ops[i]
        q = o["q"]
        kn = know.setdefault(q, {})
        w = {}
        for d in o["dep"]:
            s, v = ops[d]["done"]
            if kn.get(s, 0) < v and w.get(s, (0,))[0] < v:
                w[s] = (v, d)
        o["waits"] = []
        for s in sorted(w, key=lambda k: -ops[w[k][1]]["t0"]):
            v, d = w[s]
            if kn.get(s, 0) >= v:
                continue
            o["waits"].append((s, v))
            for a, z in ops[d]["snap"].items():
                kn[a] = max(kn.get(a, 0), z)
            kn[s] = max(kn.get(s, 0), v)
        if o["kind"] in ("arr", "dma"):
            o["done"] = (o["sem"], 16)
        elif o["kind"] in ("send", "rsend"):
            o["done"] = ("sent", 0)
        else:
            cnt[q] = cnt.get(q, 0) + 1
            o["done"] = (q, cnt[q])
        o["snap"] = dict(kn)
    return cnt


PLAN = {}


def plan():
    if not PLAN:
        ops = make_plan()
        link(ops)
        order, total, busy = schedule(ops)
        PLAN.update(ops=ops, order=order, cnt=waits(ops, order), total=total, busy=busy)
    return PLAN


def rank_program(g, core, T, topo):
    rank = T.rank_of(core)
    if rank is None:
        return
    pl = plan()
    ops = pl["ops"]
    N = len(T.cores)
    queue = {"v": g.vector, "s": g.scalar, "p": g.tensor, "q": g, "y": g.sync}

    def ap(r):
        if not isref(r):
            return r
        if r[0] == "ind":
            return ap(r[1]).indirect(ap(r[2]))
        return T[r[0]][r[3]]

    def side(r):
        if r[0] == "T":
            return T[r[1]][:, r[2]:r[3]] if len(r) > 2 else T[r[1]][:]
        return ap(r)

    nxt = T.cores[(rank + 3) % N]
    sent = [0]
    narr = {}
    for t in range(1, ROUNDS):
        for c in range(NC):
            narr["a%d_%d" % (t, c)] = len(topo.engines(T.cores[(rank - 3) % N], core))
    narr["ar"] = sum(len(topo.engines(T.cores[(rank - 3 * t) % N], core)) for t in range(1, ROUNDS))
    for i in pl["order"]:
        o = ops[i]
        k, a = o["kind"], o["args"]
        if k == "arr":
            continue
        Q = queue[o["q"]]
        for s, v in o["waits"]:
            Q.wait_ge(T.sem[s], narr.get(s, v))
        if k == "ts":
            r = Q.tensor_scalar(ap(a[0]), ap(a[1]), ap(a[2]), ap(a[3]), a[4]) if a[5] is None else \
                Q.tensor_scalar(ap(a[0]), ap(a[1]), ap(a[2]), ap(a[3]), a[4], a[5])
        elif k == "tt":
            r = Q.tensor_tensor(ap(a[0]), ap(a[1]), ap(a[2]), a[3])
        elif k == "cp":
            r = Q.tensor_copy(ap(a[0]), ap(a[1]))
        elif k == "ms":
            r = Q.memset(ap(a[0]), a[1])
        elif k == "red":
            r = Q.tensor_reduce(ap(a[0]), ap(a[1]), AxisListType.X, A.add)
        elif k == "act":
            r = Q.activation(ap(a[0]), ap(a[1]), a[2], bias=ap(a[3]), scale=a[4], accum_out=ap(a[5]))
        elif k == "mm":
            for m in a:
                r = Q.matmul(ap(m[0]), ap(m[1]), ap(m[2]), m[3], m[4])
        elif k == "iota":
            r = Q.iota(ap(a[0]), a[1], a[2], a[3], allow_small_or_imprecise_dtypes=True)
        elif k == "sel":
            r = Q.affine_select(ap(a[0]), ap(a[1]), a[2], a[3], a[4], a[5], a[6])
        elif k == "dma":
            Q.dma_start(side(a[0]), side(a[1])).then_inc(T.sem[o["sem"]], 16)
            continue
        elif k == "send":
            rid, pid = topo.addr(nxt, core)
            src = R("sd", 256 * a[0] + n * a[1], 256 * a[0] + n * a[1] + n)
            dst = R("rf", 256 * (a[0] + 1) + n * a[1], 256 * (a[0] + 1) + n * a[1] + n)
            Q.remote_dma(ap(dst), ap(src), T.sem["a%d_%d" % (a[0] + 1, a[1])], T.sem["sent"], pid, rid, topo.mask(core, nxt))
            sent[0] += len(topo.engines(core, nxt))
            continue
        else:
            ids, dsts = [], []
            for t in range(1, ROUNDS):
                d = T.cores[(rank + 3 * t) % N]
                rid, pid = topo.addr(d, core)
                ids.append(DstId(rid=rid, pnc=pid))
                dsts.append(ap(R("rr", 16 * t, 16 * t + 16)))
            Q.remote_dma_fused([RemoteDMATransfer(dst_ids=ids, dma_engine_mask=topo.mask(core, nxt), remote_sem=T.sem["ar"],
                                                  srcs=[ap(R("rr", 0, 16))], dsts=dsts)], local_sem=T.sem["sent"])
            sent[0] += len(topo.engines(core, nxt))
            continue
        r.then_inc(T.sem[o["q"]], 1)
    for s in sorted(pl["cnt"]):
        g.wait_ge(T.sem[s], pl["cnt"][s])
    g.wait_ge(T.sem["sent"], sent[0])
    for s in ("dr", "dx", "dc", "oy0", "oy1", "oc"):
        g.sync.wait_ge(T.sem[s], 16)
